import numpy as np
import ml_dtypes


def mxq(x, axis, fmt="e4m3"):
    dtype, down = {"e4m3": (ml_dtypes.float8_e4m3fn, 7), "e5m2": (ml_dtypes.float8_e5m2, 14)}[fmt]
    v = np.moveaxis(np.asarray(x, np.float32).astype(ml_dtypes.bfloat16).astype(np.float64), axis, -1)
    blocks = v.reshape(v.shape[:-1] + (-1, 32))
    amax = np.abs(blocks).max(-1, keepdims=True)
    byte = np.maximum(np.where(amax > 0, np.frexp(amax)[1] - 1 + 127, 0) - down, 1)
    scale = np.exp2(byte - 127.0)
    codes = (blocks / scale).astype(np.float32).astype(dtype).astype(np.float64)
    return np.moveaxis((codes * scale).reshape(v.shape), -1, axis)


WIDE = False


def mx_kscale(k):
    if not WIDE:
        return np.ones(k)
    levels = np.array([24, -24, 12, -12, 0])
    if k % 512:
        return np.exp2(np.random.permutation(np.resize(levels, k // 32))).repeat(32)
    a = np.empty((k // 512, 16))
    for p in range(k // 512):
        a[p, :8] = np.random.permutation(np.resize(levels, 8))
        for g in range(8):
            far = levels[np.abs(levels - a[p, g]) >= 10]
            a[p, g + 8] = far[np.random.randint(len(far))]
    return np.exp2(a.ravel()).repeat(32)


def f64(x):
    return np.asarray(x).astype(np.float64)


def striped(idx):
    return np.tile(idx.reshape(-1, 16).T, (8, 1)).astype(np.uint16)


def unstriped(offs):
    return offs[:16].T.reshape(-1).astype(np.int64)


E2M1 = np.array([0.0, 0.5, 1.0, 1.5, 2.0, 3.0, 4.0, 6.0, -0.0, -0.5, -1.0, -1.5, -2.0, -3.0, -4.0, -6.0])


def pack_weight(w, fmt):
    k, n = w.shape
    w = f64(np.asarray(w, np.float32).astype(ml_dtypes.bfloat16)).reshape(k // 32, 32, n)
    amax = np.abs(w).max(1)
    if fmt == "e4m3":
        byte = np.frexp(amax)[1] - 1 + 127 - 7
    else:
        mant, ex = np.frexp(amax / 6.0)
        byte = np.where(mant > 0.5, ex, ex - 1) + 127
    byte = np.clip(np.where(amax > 0, byte, 1), 1, 254)
    scaled = (w * np.exp2(127.0 - byte)[:, None, :]).reshape(k, n).astype(np.float32)
    by_word = np.ascontiguousarray(scaled.reshape(k // 512, 128, 4, n).transpose(0, 1, 3, 2))
    if fmt == "e4m3":
        words = by_word.astype(ml_dtypes.float8_e4m3fn).view(np.uint8)
    else:
        c = by_word.astype(ml_dtypes.float4_e2m1fn).view(np.uint8) & 0xF
        words = (c[..., 0::2] | (c[..., 1::2] << 4)).reshape(k // 512, 128, 2 * n)
    return np.ascontiguousarray(words), np.ascontiguousarray(byte.astype(np.uint8).reshape(k // 512, 16, n))


def unpack_weight(words, scales, fmt):
    g, _, n = scales.shape
    words = np.ascontiguousarray(words).reshape(g, 128, n, -1)
    if fmt == "e4m3":
        vals = words.view(ml_dtypes.float8_e4m3fn).astype(np.float64)
    else:
        nib = np.empty((g, 128, n, 4), np.uint8)
        nib[..., 0::2] = words & 0xF
        nib[..., 1::2] = words >> 4
        vals = E2M1[nib]
    vals = vals * np.repeat(np.exp2(scales.astype(np.float64) - 127.0), 8, axis=1)[..., None]
    return vals.transpose(0, 1, 3, 2).reshape(g * 512, n)


K, F, N, T, J = 512, 1024, 256, 2048, 1024


def setup_inputs():
    n = np.random.standard_normal
    s = mx_kscale(K)[:, None]
    u = mx_kscale(F)[:, None]
    fb = np.abs(n((F, N))) / F / u
    p_tab = pack_weight(n((K, T)) * s, "e4m3")
    p_fb8 = pack_weight(fb[:512], "e4m3")
    p_fb4 = pack_weight(fb[512:], "e2m1")
    return {
        "tab_words": p_tab[0],
        "tab_scales": p_tab[1],
        "co": (n((K, F)) / np.sqrt(K) / s).astype(np.float32),
        "si": (n((K, F)) / np.sqrt(K) / s).astype(np.float32),
        "gn": (np.random.uniform(0.5, 2.0, F) * u[:, 0]).astype(np.float32),
        "fb8_words": p_fb8[0],
        "fb8_scales": p_fb8[1],
        "fb4_words": p_fb4[0],
        "fb4_scales": p_fb4[1],
        "offs": striped(np.random.permutation(T)[:J]),
    }


def reference(tab_words, tab_scales, co, si, gn, fb8_words, fb8_scales, fb4_words, fb4_scales, offs):
    idx = unstriped(offs)
    tab_ = unpack_weight(tab_words, tab_scales, "e4m3")[:, idx]
    co_ = mxq(f64(co), 0, "e4m3")
    si_ = mxq(f64(si), 0, "e4m3")
    re = co_.T @ tab_
    im = si_.T @ tab_
    h = f64(gn)[:, None] * ((re) ** 2 + (im) ** 2)
    h_ = mxq(h, 0, "e4m3")
    fb8_ = unpack_weight(fb8_words, fb8_scales, "e4m3")
    fb4_ = unpack_weight(fb4_words, fb4_scales, "e2m1")
    y = fb8_.T @ h_[:512] + fb4_.T @ h_[512:]
    return y

@@ -1,0 +1,252 @@
+from contextlib import ExitStack
+
+import concourse.mybir as mybir
+
+K, F, N, T, J = 512, 1024, 256, 2048, 1024
+FLOPS = 2 * (2 * K * F * J + F * N * J)
+
+F32 = mybir.dt.float32
+BF16 = mybir.dt.bfloat16
+I32 = mybir.dt.int32
+U32 = mybir.dt.uint32
+U16 = mybir.dt.uint16
+U8 = mybir.dt.uint8
+FP8X4 = mybir.dt.float8_e4m3fn_x4
+FP4X4 = mybir.dt.float4_e2m1fn_x4
+ACT = mybir.ActivationFunctionType
+ALU = mybir.AluOpType
+
+P = 128
+PACK = 4
+PASS = P * PACK
+LINE = 4
+GATHER = 512
+GROUP = 128
+PICKS = 256
+UNITS = [(0, 0, 256), (0, 256, 256), (0, 512, 256), (0, 768, 256), (1, 0, 256), (1, 256, 256), (1, 512, 256), (1, 768, 128), (1, 896, 128)]
+SCALAR_CASTS = {("co", 0, 0), ("co", 0, 1), ("si", 1, 0)}
+VECTOR_OUTS = {896}
+
+
+def load_scale_rows(queue, plane, rows):
+    for quad in range(4):
+        queue.dma_start(out=plane[32 * quad : 32 * quad + 4, :], in_=rows[4 * quad : 4 * quad + 4, :].bitcast(I32))
+
+
+def tile_list_meltab_mix_pow_kernel(
+    tc, tab_words, tab_scales, co, si, gn, fb8_words, fb8_scales, fb4_words, fb4_scales, offs, out
+):
+    nc = tc.nc
+    with ExitStack() as ctx:
+        keep = ctx.enter_context(tc.tile_pool(name="keep", bufs=1))
+        sums = ctx.enter_context(tc.psum_pool(name="sums", bufs=6))
+        results = ctx.enter_context(tc.psum_pool(name="results", bufs=2))
+
+        offsets = keep.tile([P, J // 16], U16, name="offsets")
+        table = keep.tile([P, T], I32, name="table", align_bytes=64)
+        table_plane = keep.tile([P, T // 4], I32, name="table_plane", align_bytes=64)
+        fb_plane = keep.tile([P, 2 * N // 4], I32, name="fb_plane", align_bytes=64)
+        fb8 = keep.tile([P, N], I32, name="fb8", align_bytes=64)
+        fb4 = keep.tile([P, N // 2], I32, name="fb4", align_bytes=64)
+        gain = keep.tile([P, 2, PACK], F32, name="gain")
+
+        nc.vector.memset(table_plane[:], 0)
+        nc.vector.memset(fb_plane[:], 0)
+        nc.sync.dma_start(out=table[:], in_=tab_words[0].rearrange("p t i -> p (t i)").bitcast(I32))
+        nc.sync.dma_start(offsets[:], offs)
+        load_scale_rows(nc.scalar, table_plane, tab_scales[0])
+        nc.scalar.dma_start(out=gain[:], in_=gn.rearrange("(b p t) -> p b t", b=2, t=PACK))
+
+        weights = {"co": co, "si": si}
+        raw = {}
+        for b in range(2):
+            for name in ("co", "si"):
+                for half in range(2):
+                    raw[name, b, half] = keep.tile([P, PACK, PASS // 2], F32, name="raw_%s%d%d" % (name, b, half))
+                    f0 = b * PASS + half * PASS // 2
+                    nc.sync.dma_start(
+                        out=raw[name, b, half][:],
+                        in_=weights[name].rearrange("(p i) f -> p i f", i=PACK)[:, :, f0 : f0 + PASS // 2],
+                    )
+        nc.sync.dma_start(out=fb8[:], in_=fb8_words[0].rearrange("p n i -> p (n i)").bitcast(I32))
+        nc.sync.dma_start(out=fb4[:], in_=fb4_words[0].bitcast(I32))
+        load_scale_rows(nc.sync, fb_plane[:, : N // 4], fb8_scales[0])
+        load_scale_rows(nc.sync, fb_plane[:, N // 4 :], fb4_scales[0])
+
+        flat_gain = gain[:].rearrange("p b t -> p (b t)")
+        size = keep.tile([P, 2 * PACK], F32, name="size")
+        half_power = keep.tile([P, 2 * PACK], F32, name="half_power")
+        root = keep.tile([P, 2 * PACK], F32, name="root")
+        sign = keep.tile([P, 2 * PACK], BF16, name="sign")
+        nc.gpsimd.memset(half_power[:], 0.5)
+        nc.scalar.activation(size[:], flat_gain, ACT.Abs)
+        nc.scalar.activation(sign[:], flat_gain, ACT.Sign)
+        nc.gpsimd.tensor_tensor(root[:], size[:], half_power[:], ALU.pow)
+
+        frames = {}
+
+        def gather(piece):
+            words = keep.tile([P, GATHER], U32, name="frame_words%d" % piece, align_bytes=64)
+            plane = keep.tile([P, GATHER], U8, name="frame_plane%d" % piece, align_bytes=64)
+            for j0 in range(0, GATHER, PICKS):
+                first = piece * GATHER + j0
+                picks = offsets[:, first // 16 : (first + PICKS) // 16]
+                nc.vector.tensor_copy(words[:, j0 : j0 + PICKS], table[:].bitcast(U32).indirect(picks))
+                nc.vector.tensor_copy(plane[:, j0 : j0 + PICKS], table_plane[:].bitcast(U8).indirect(picks))
+            frames[piece] = (words, plane)
+
+        packed = {}
+
+        def quantize_weight(name, b):
+            grouped = keep.tile([P, PACK, P, PACK], BF16, name="grouped_%s%d" % (name, b), align_bytes=64)
+            for half in range(2):
+                dst = grouped[:, :, half * P // 2 : (half + 1) * P // 2, :].rearrange("p t m i -> p m i t")
+                src = raw[name, b, half][:].rearrange("p i (m t) -> p m i t", t=PACK)
+                if (name, b, half) in SCALAR_CASTS:
+                    nc.scalar.copy(dst, src)
+                else:
+                    nc.vector.tensor_copy(dst, src)
+            words = keep.tile([P, PASS], U32, name="words_%s%d" % (name, b), align_bytes=64)
+            plane = keep.tile([P, PASS], U8, name="plane_%s%d" % (name, b), align_bytes=64)
+            step = 1 if b == 0 else PACK
+            for t in range(0, PACK, step):
+                nc.vector.quantize_mx(
+                    out=words[:, t * P : (t + step) * P].bitcast(FP8X4),
+                    scales=plane[:, t * P : (t + step) * P],
+                    in_=grouped[:, t : t + step].rearrange("p t m i -> p (t m i)"),
+                )
+            packed[name, b] = (words, plane)
+
+        def transform(bank_cols, name, b, t, j0, width):
+            w_words, w_plane = packed[name, b]
+            x_words, x_plane = frames[j0 // GATHER]
+            cols = slice(j0 % GATHER, j0 % GATHER + width)
+            nc.tensor.matmul_mx(
+                out=bank_cols,
+                lhsT=w_words[:, t * P : (t + 1) * P].bitcast(FP8X4),
+                lhsT_scale=w_plane[:, t * P : (t + 1) * P],
+                rhs=x_words[:, cols].bitcast(FP8X4),
+                rhs_scale=x_plane[:, cols],
+                start=True,
+                stop=True,
+            )
+
+        squares = {}
+
+        def square_part(name, b, j0, width):
+            if (b, j0) not in squares:
+                squares[b, j0] = keep.tile([P, PACK, 2, width], F32, name="squares%d_%d" % (b, j0))
+            for t in range(PACK):
+                bank = sums.tile([P, PASS], F32, name="bank")
+                transform(bank[:, :width], name, b, t, j0, width)
+                nc.scalar.activation(
+                    squares[b, j0][:, t, ("co", "si").index(name), :],
+                    bank[:, :width],
+                    ACT.Square,
+                    scale=root[:, b * PACK + t : b * PACK + t + 1],
+                )
+
+        def square_both(b, j0, width):
+            squares[b, j0] = keep.tile([P, PACK, 2, width], F32, name="squares%d_%d" % (b, j0))
+            for t in range(PACK):
+                bank = sums.tile([P, PASS], F32, name="bank")
+                transform(bank[:, :width], "co", b, t, j0, width)
+                transform(bank[:, width : 2 * width], "si", b, t, j0, width)
+                nc.scalar.activation(
+                    squares[b, j0][:, t].rearrange("p s j -> p (s j)"),
+                    bank[:, : 2 * width],
+                    ACT.Square,
+                    scale=root[:, b * PACK + t : b * PACK + t + 1],
+                )
+
+        unsigned = {}
+        signed = {}
+
+        def add(b, j0, width, base):
+            tile = keep.tile([P, width, PACK], BF16, name="unsigned%d_%d" % (b, j0), align_bytes=64)
+            cols = slice(j0 - base, j0 - base + width)
+            nc.vector.tensor_tensor(
+                tile[:].rearrange("p (c i) t -> p c t i", i=LINE),
+                squares[b, base][:, :, 0, cols].rearrange("p t (c i) -> p c t i", i=LINE),
+                squares[b, base][:, :, 1, cols].rearrange("p t (c i) -> p c t i", i=LINE),
+                ALU.add,
+            )
+            unsigned[b, j0] = tile
+
+        def apply_sign(b, j0, width):
+            tile = keep.tile([P, width, PACK], BF16, name="signed%d_%d" % (b, j0), align_bytes=64)
+            nc.vector.tensor_tensor(
+                tile[:],
+                unsigned[b, j0][:],
+                sign[:, b * PACK : (b + 1) * PACK].unsqueeze(1).to_broadcast([P, width, PACK]),
+                ALU.mult,
+            )
+            signed[b, j0] = tile
+
+        power_words = [keep.tile([P, J], U32, name="power_words%d" % b, align_bytes=64) for b in range(2)]
+        power_plane = [keep.tile([P, J], U8, name="power_plane%d" % b, align_bytes=64) for b in range(2)]
+
+        def quantize_power(b, j0, width):
+            nc.vector.quantize_mx(
+                out=power_words[b][:, j0 : j0 + width].bitcast(FP8X4),
+                scales=power_plane[b][:, j0 : j0 + width],
+                in_=signed[b, j0][:].rearrange("p j t -> p (j t)"),
+            )
+
+        fb_bytes = fb_plane[:].bitcast(U8)
+
+        def filter_bank(j0, width):
+            acc = results.tile([P, PASS], F32, name="acc")
+            for nt in range(N // P):
+                for g0 in range(0, width, GROUP):
+                    cols = slice(j0 + g0, j0 + g0 + GROUP)
+                    dst = acc[:, nt * width + g0 : nt * width + g0 + GROUP]
+                    nc.tensor.matmul_mx(
+                        out=dst,
+                        lhsT=fb8[:, nt * P : (nt + 1) * P].bitcast(FP8X4),
+                        lhsT_scale=fb_bytes[:, nt * P : (nt + 1) * P],
+                        rhs=power_words[0][:, cols].bitcast(FP8X4),
+                        rhs_scale=power_plane[0][:, cols],
+                        start=True,
+                        stop=False,
+                    )
+                    nc.tensor.matmul_mx(
+                        out=dst,
+                        lhsT=fb4[:].bitcast(U8)[:, nt * 2 * P : (nt + 1) * 2 * P].bitcast(FP4X4),
+                        lhsT_scale=fb_bytes[:, N + nt * P : N + (nt + 1) * P],
+                        rhs=power_words[1][:, cols].bitcast(FP8X4),
+                        rhs_scale=power_plane[1][:, cols],
+                        start=False,
+                        stop=True,
+                    )
+            staged = keep.tile([P, N // P, width], F32, name="staged%d" % j0)
+            flat = staged[:].rearrange("p a j -> p (a j)")
+            if j0 in VECTOR_OUTS:
+                nc.vector.tensor_copy(flat, acc[:, : 2 * width])
+            else:
+                nc.scalar.copy(flat, acc[:, : 2 * width])
+            nc.sync.dma_start(out=out.rearrange("(a p) j -> p a j", p=P)[:, :, j0 : j0 + width], in_=staged[:])
+
+        gather(0)
+        quantize_weight("co", 0)
+        square_part("co", 0, 0, GATHER)
+        quantize_weight("si", 0)
+        gather(1)
+        square_part("si", 0, 0, GATHER)
+        quantize_weight("co", 1)
+        quantize_weight("si", 1)
+
+        for step in range(len(UNITS) + 2):
+            if step < len(UNITS):
+                b, j0, width = UNITS[step]
+                early = b == 0 and j0 < GATHER
+                if not early:
+                    square_both(b, j0, width)
+                add(b, j0, width, 0 if early else j0)
+            if 1 <= step <= len(UNITS):
+                apply_sign(*UNITS[step - 1])
+            if step >= 2:
+                b, j0, width = UNITS[step - 2]
+                quantize_power(b, j0, width)
+                if b == 1:
+                    filter_bank(j0, width)

@@ -1,6 +1,7 @@
 from contextlib import ExitStack
 
 import concourse.mybir as mybir
+from concourse.masks import make_identity
 
 K, F, N, T, J = 512, 1024, 256, 2048, 1024
 FLOPS = 2 * (2 * K * F * J + F * N * J)
@@ -20,11 +21,9 @@ P = 128
 PACK = 4
 PASS = P * PACK
 LINE = 4
-GATHER = 512
 GROUP = 128
-PICKS = 256
-UNITS = [(0, 0, 256), (0, 256, 256), (0, 512, 256), (0, 768, 256), (1, 0, 256), (1, 256, 256), (1, 512, 256), (1, 768, 128), (1, 896, 128)]
-SCALAR_CASTS = {("co", 0, 0), ("co", 0, 1), ("si", 1, 0)}
+LOW_WIDTH = 512
+UNITS = [(0, 512, 512), (1, 0, 256), (1, 256, 256), (1, 512, 256), (1, 768, 128), (1, 896, 128)]
 VECTOR_OUTS = {896}
 
 
@@ -39,8 +38,8 @@ def tile_list_meltab_mix_pow_kernel(
     nc = tc.nc
     with ExitStack() as ctx:
         keep = ctx.enter_context(tc.tile_pool(name="keep", bufs=1))
-        sums = ctx.enter_context(tc.psum_pool(name="sums", bufs=6))
-        results = ctx.enter_context(tc.psum_pool(name="results", bufs=2))
+        sums = ctx.enter_context(tc.psum_pool(name="sums", bufs=4))
+        results = ctx.enter_context(tc.psum_pool(name="results", bufs=4))
 
         offsets = keep.tile([P, J // 16], U16, name="offsets")
         table = keep.tile([P, T], I32, name="table", align_bytes=64)
@@ -52,27 +51,35 @@ def tile_list_meltab_mix_pow_kernel(
 
         nc.vector.memset(table_plane[:], 0)
         nc.vector.memset(fb_plane[:], 0)
-        nc.sync.dma_start(out=table[:], in_=tab_words[0].rearrange("p t i -> p (t i)").bitcast(I32))
-        nc.sync.dma_start(offsets[:], offs)
-        load_scale_rows(nc.scalar, table_plane, tab_scales[0])
-        nc.scalar.dma_start(out=gain[:], in_=gn.rearrange("(b p t) -> p b t", b=2, t=PACK))
-
         weights = {"co": co, "si": si}
         raw = {}
-        for b in range(2):
-            for name in ("co", "si"):
-                for half in range(2):
-                    raw[name, b, half] = keep.tile([P, PACK, PASS // 2], F32, name="raw_%s%d%d" % (name, b, half))
-                    f0 = b * PASS + half * PASS // 2
-                    nc.sync.dma_start(
-                        out=raw[name, b, half][:],
-                        in_=weights[name].rearrange("(p i) f -> p i f", i=PACK)[:, :, f0 : f0 + PASS // 2],
-                    )
+
+        def load_weight(name, b):
+            raw[name, b] = keep.tile([P, PACK, PASS], F32, name="raw_%s%d" % (name, b))
+            nc.sync.dma_start(
+                out=raw[name, b][:],
+                in_=weights[name].rearrange("(p i) f -> p i f", i=PACK)[:, :, b * PASS : (b + 1) * PASS],
+            )
+
+        nc.sync.dma_start(offsets[:], offs)
+        raw["co", 0] = keep.tile([P, PACK, PASS], F32, name="raw_co0")
+        co_rows = co.rearrange("(p i) f -> p i f", i=PACK)
+        nc.sync.dma_start(out=raw["co", 0][:, :2], in_=co_rows[:, :2, :PASS])
+        load_scale_rows(nc.sync, table_plane, tab_scales[0])
+        nc.sync.dma_start(out=raw["co", 0][:, 2:], in_=co_rows[:, 2:, :PASS])
+        nc.sync.dma_start(out=table[:], in_=tab_words[0].rearrange("p t i -> p (t i)").bitcast(I32))
+
+        nc.sync.dma_start(out=gain[:], in_=gn.rearrange("(b p t) -> p b t", b=2, t=PACK))
+        load_weight("si", 0)
+        load_weight("co", 1)
+        load_weight("si", 1)
         nc.sync.dma_start(out=fb8[:], in_=fb8_words[0].rearrange("p n i -> p (n i)").bitcast(I32))
         nc.sync.dma_start(out=fb4[:], in_=fb4_words[0].bitcast(I32))
         load_scale_rows(nc.sync, fb_plane[:, : N // 4], fb8_scales[0])
         load_scale_rows(nc.sync, fb_plane[:, N // 4 :], fb4_scales[0])
 
+        identity = keep.tile([P, P], F32, name="identity")
+        make_identity(nc, identity[:])
         flat_gain = gain[:].rearrange("p b t -> p (b t)")
         size = keep.tile([P, 2 * PACK], F32, name="size")
         half_power = keep.tile([P, 2 * PACK], F32, name="half_power")
@@ -83,78 +90,123 @@ def tile_list_meltab_mix_pow_kernel(
         nc.scalar.activation(sign[:], flat_gain, ACT.Sign)
         nc.gpsimd.tensor_tensor(root[:], size[:], half_power[:], ALU.pow)
 
-        frames = {}
+        frame_words = keep.tile([P, J], U32, name="frame_words", align_bytes=64)
+        frame_plane = keep.tile([P, J], U8, name="frame_plane", align_bytes=64)
 
-        def gather(piece):
-            words = keep.tile([P, GATHER], U32, name="frame_words%d" % piece, align_bytes=64)
-            plane = keep.tile([P, GATHER], U8, name="frame_plane%d" % piece, align_bytes=64)
-            for j0 in range(0, GATHER, PICKS):
-                first = piece * GATHER + j0
-                picks = offsets[:, first // 16 : (first + PICKS) // 16]
-                nc.vector.tensor_copy(words[:, j0 : j0 + PICKS], table[:].bitcast(U32).indirect(picks))
-                nc.vector.tensor_copy(plane[:, j0 : j0 + PICKS], table_plane[:].bitcast(U8).indirect(picks))
-            frames[piece] = (words, plane)
+        def gather(dst, window, j0, width):
+            picks = offsets[:, j0 // 16 : (j0 + width) // 16]
+            nc.vector.tensor_copy(dst[:, j0 : j0 + width], window.indirect(picks))
 
+        def gather_words(j0, width):
+            gather(frame_words, table[:].bitcast(U32), j0, width)
+
+        def gather_scales(j0, width):
+            gather(frame_plane, table_plane[:].bitcast(U8), j0, width)
+
+        grouped = {}
         packed = {}
 
-        def quantize_weight(name, b):
-            grouped = keep.tile([P, PACK, P, PACK], BF16, name="grouped_%s%d" % (name, b), align_bytes=64)
-            for half in range(2):
-                dst = grouped[:, :, half * P // 2 : (half + 1) * P // 2, :].rearrange("p t m i -> p m i t")
-                src = raw[name, b, half][:].rearrange("p i (m t) -> p m i t", t=PACK)
-                if (name, b, half) in SCALAR_CASTS:
-                    nc.scalar.copy(dst, src)
-                else:
-                    nc.vector.tensor_copy(dst, src)
+        def cast_weight(engine_copy, name, b, half):
+            if (name, b) not in grouped:
+                grouped[name, b] = keep.tile(
+                    [P, PACK, P, PACK], BF16, name="grouped_%s%d" % (name, b), align_bytes=64
+                )
+            slots = slice(2 * half, 2 * half + 2)
+            dst = grouped[name, b][:].rearrange("p t m i -> p m i t")
+            src = raw[name, b][:].rearrange("p i (m t) -> p m i t", t=PACK)
+            engine_copy(dst[:, :, :, slots], src[:, :, :, slots])
+
+        def quantize_weight(name, b, pieces=2):
             words = keep.tile([P, PASS], U32, name="words_%s%d" % (name, b), align_bytes=64)
             plane = keep.tile([P, PASS], U8, name="plane_%s%d" % (name, b), align_bytes=64)
-            step = 1 if b == 0 else PACK
+            step = PACK // pieces
             for t in range(0, PACK, step):
                 nc.vector.quantize_mx(
                     out=words[:, t * P : (t + step) * P].bitcast(FP8X4),
                     scales=plane[:, t * P : (t + step) * P],
-                    in_=grouped[:, t : t + step].rearrange("p t m i -> p (t m i)"),
+                    in_=grouped[name, b][:, t : t + step].rearrange("p t m i -> p (t m i)"),
                 )
             packed[name, b] = (words, plane)
 
         def transform(bank_cols, name, b, t, j0, width):
             w_words, w_plane = packed[name, b]
-            x_words, x_plane = frames[j0 // GATHER]
-            cols = slice(j0 % GATHER, j0 % GATHER + width)
+            cols = slice(j0, j0 + width)
             nc.tensor.matmul_mx(
                 out=bank_cols,
                 lhsT=w_words[:, t * P : (t + 1) * P].bitcast(FP8X4),
                 lhsT_scale=w_plane[:, t * P : (t + 1) * P],
-                rhs=x_words[:, cols].bitcast(FP8X4),
-                rhs_scale=x_plane[:, cols],
+                rhs=frame_words[:, cols].bitcast(FP8X4),
+                rhs_scale=frame_plane[:, cols],
                 start=True,
                 stop=True,
             )
 
         squares = {}
 
-        def square_part(name, b, j0, width):
-            if (b, j0) not in squares:
-                squares[b, j0] = keep.tile([P, PACK, 2, width], F32, name="squares%d_%d" % (b, j0))
+        def square_tile(b, j0, width):
+            squares[b, j0] = keep.tile([P, 2, width // LINE, PACK, LINE], F32, name="squares%d_%d" % (b, j0))
+
+        def square_part(name, b, base, j0, width):
+            rows = slice((j0 - base) // LINE, (j0 - base + width) // LINE)
             for t in range(PACK):
                 bank = sums.tile([P, PASS], F32, name="bank")
                 transform(bank[:, :width], name, b, t, j0, width)
                 nc.scalar.activation(
-                    squares[b, j0][:, t, ("co", "si").index(name), :],
-                    bank[:, :width],
+                    squares[b, base][:, ("co", "si").index(name), rows, t, :],
+                    bank[:, :width].rearrange("p (c i) -> p c i", i=LINE),
                     ACT.Square,
                     scale=root[:, b * PACK + t : b * PACK + t + 1],
                 )
 
+        by_frame = {}
+
+        def square_by_frame(name, jt):
+            w_words, w_plane = packed[name, 0]
+            cols = slice(jt * P, (jt + 1) * P)
+            bank = sums.tile([P, PASS], F32, name="bank")
+            nc.tensor.matmul_mx(
+                out=bank[:],
+                lhsT=frame_words[:, cols].bitcast(FP8X4),
+                lhsT_scale=frame_plane[:, cols],
+                rhs=w_words[:].bitcast(FP8X4),
+                rhs_scale=w_plane[:],
+                start=True,
+                stop=True,
+            )
+            by_frame[name, jt] = keep.tile([P, PASS], F32, name="by_frame_%s%d" % (name, jt))
+            nc.scalar.activation(by_frame[name, jt][:], bank[:], ACT.Square)
+
+        def turn_and_scale(jt):
+            bank = results.tile([P, PACK, P], F32, name="acc")
+            for t in range(PACK):
+                for name in ("co", "si"):
+                    nc.tensor.matmul(
+                        bank[:, t, :],
+                        by_frame[name, jt][:, t * P : (t + 1) * P],
+                        identity[:],
+                        start=name == "co",
+                        stop=name == "si",
+                        is_transpose=True,
+                    )
+            j0 = jt * P - jt * P % LOW_WIDTH
+            if (0, j0) not in signed:
+                signed[0, j0] = keep.tile([P, LOW_WIDTH, PACK], BF16, name="signed0_%d" % j0, align_bytes=64)
+            nc.vector.tensor_tensor(
+                signed[0, j0][:, jt * P - j0 : (jt + 1) * P - j0, :],
+                bank[:].rearrange("p t j -> p j t"),
+                gain[:, 0].unsqueeze(1).to_broadcast([P, P, PACK]),
+                ALU.mult,
+            )
+
         def square_both(b, j0, width):
-            squares[b, j0] = keep.tile([P, PACK, 2, width], F32, name="squares%d_%d" % (b, j0))
+            square_tile(b, j0, width)
             for t in range(PACK):
                 bank = sums.tile([P, PASS], F32, name="bank")
                 transform(bank[:, :width], "co", b, t, j0, width)
                 transform(bank[:, width : 2 * width], "si", b, t, j0, width)
                 nc.scalar.activation(
-                    squares[b, j0][:, t].rearrange("p s j -> p (s j)"),
-                    bank[:, : 2 * width],
+                    squares[b, j0][:, :, :, t, :].rearrange("p s c i -> p (s c) i"),
+                    bank[:, : 2 * width].rearrange("p (c i) -> p c i", i=LINE),
                     ACT.Square,
                     scale=root[:, b * PACK + t : b * PACK + t + 1],
                 )
@@ -162,13 +214,14 @@ def tile_list_meltab_mix_pow_kernel(
         unsigned = {}
         signed = {}
 
-        def add(b, j0, width, base):
+        def add(b, j0, width):
             tile = keep.tile([P, width, PACK], BF16, name="unsigned%d_%d" % (b, j0), align_bytes=64)
-            cols = slice(j0 - base, j0 - base + width)
+            base = max(start for (half, start) in squares if half == b and start <= j0)
+            rows = slice((j0 - base) // LINE, (j0 - base + width) // LINE)
             nc.vector.tensor_tensor(
                 tile[:].rearrange("p (c i) t -> p c t i", i=LINE),
-                squares[b, base][:, :, 0, cols].rearrange("p t (c i) -> p c t i", i=LINE),
-                squares[b, base][:, :, 1, cols].rearrange("p t (c i) -> p c t i", i=LINE),
+                squares[b, base][:, 0, rows],
+                squares[b, base][:, 1, rows],
                 ALU.add,
             )
             unsigned[b, j0] = tile
@@ -227,22 +280,40 @@ def tile_list_meltab_mix_pow_kernel(
                 nc.scalar.copy(flat, acc[:, : 2 * width])
             nc.sync.dma_start(out=out.rearrange("(a p) j -> p a j", p=P)[:, :, j0 : j0 + width], in_=staged[:])
 
-        gather(0)
-        quantize_weight("co", 0)
-        square_part("co", 0, 0, GATHER)
+        gather_scales(0, 1024)
+        cast_weight(nc.vector.tensor_copy, "co", 0, 0)
+        cast_weight(nc.vector.tensor_copy, "co", 0, 1)
+        quantize_weight("co", 0, 2)
+        gather_words(0, 256)
+        gather_words(256, 256)
+        gather_words(512, 512)
+        for jt in range(LOW_WIDTH // P):
+            square_by_frame("co", jt)
+        square_tile(0, 512, 512)
+        square_part("co", 0, 512, 512, 512)
+        cast_weight(nc.vector.tensor_copy, "si", 0, 0)
+        cast_weight(nc.vector.tensor_copy, "si", 0, 1)
         quantize_weight("si", 0)
-        gather(1)
-        square_part("si", 0, 0, GATHER)
+        for jt in range(LOW_WIDTH // P):
+            square_by_frame("si", jt)
+        cast_weight(nc.vector.tensor_copy, "co", 1, 0)
+        cast_weight(nc.vector.tensor_copy, "co", 1, 1)
         quantize_weight("co", 1)
+        cast_weight(nc.vector.tensor_copy, "si", 1, 0)
+        cast_weight(nc.scalar.copy, "si", 1, 1)
+        square_part("si", 0, 512, 512, 512)
         quantize_weight("si", 1)
+        for jt in range(LOW_WIDTH // P):
+            turn_and_scale(jt)
 
         for step in range(len(UNITS) + 2):
             if step < len(UNITS):
                 b, j0, width = UNITS[step]
-                early = b == 0 and j0 < GATHER
-                if not early:
-                    square_both(b, j0, width)
-                add(b, j0, width, 0 if early else j0)
+                if b == 1 and j0 % 256 == 0:
+                    square_both(b, j0, 256)
+                add(b, j0, width)
+            if step == 0:
+                quantize_power(0, 0, LOW_WIDTH)
             if 1 <= step <= len(UNITS):
                 apply_sign(*UNITS[step - 1])
             if step >= 2:

@@ -22,9 +22,7 @@ PACK = 4
 PASS = P * PACK
 LINE = 4
 GROUP = 128
-LOW_WIDTH = 512
-UNITS = [(0, 512, 512), (1, 0, 256), (1, 256, 256), (1, 512, 256), (1, 768, 128), (1, 896, 128)]
-VECTOR_OUTS = {896}
+VECTOR_OUTS = {384}
 
 
 def load_scale_rows(queue, plane, rows):
@@ -62,14 +60,14 @@ def tile_list_meltab_mix_pow_kernel(
             )
 
         nc.sync.dma_start(offsets[:], offs)
-        raw["co", 0] = keep.tile([P, PACK, PASS], F32, name="raw_co0")
-        co_rows = co.rearrange("(p i) f -> p i f", i=PACK)
-        nc.sync.dma_start(out=raw["co", 0][:, :2], in_=co_rows[:, :2, :PASS])
-        load_scale_rows(nc.sync, table_plane, tab_scales[0])
-        nc.sync.dma_start(out=raw["co", 0][:, 2:], in_=co_rows[:, 2:, :PASS])
-        nc.sync.dma_start(out=table[:], in_=tab_words[0].rearrange("p t i -> p (t i)").bitcast(I32))
-
         nc.sync.dma_start(out=gain[:], in_=gn.rearrange("(b p t) -> p b t", b=2, t=PACK))
+        load_scale_rows(nc.sync, table_plane, tab_scales[0])
+        co_rows = co.rearrange("(p i) f -> p i f", i=PACK)
+        first = []
+        for half in range(2):
+            first.append(keep.tile([P, PACK, PASS // 2], F32, name="raw_co0_%d" % half))
+            nc.sync.dma_start(out=first[half][:], in_=co_rows[:, :, half * 256 : (half + 1) * 256])
+        nc.sync.dma_start(out=table[:], in_=tab_words[0].rearrange("p t i -> p (t i)").bitcast(I32))
         load_weight("si", 0)
         load_weight("co", 1)
         load_weight("si", 1)
@@ -116,6 +114,12 @@ def tile_list_meltab_mix_pow_kernel(
             src = raw[name, b][:].rearrange("p i (m t) -> p m i t", t=PACK)
             engine_copy(dst[:, :, :, slots], src[:, :, :, slots])
 
+        def cast_first(engine_copy, half):
+            if ("co", 0) not in grouped:
+                grouped["co", 0] = keep.tile([P, PACK, P, PACK], BF16, name="grouped_co0", align_bytes=64)
+            dst = grouped["co", 0][:, :, half * 64 : (half + 1) * 64, :].rearrange("p t m i -> p m i t")
+            engine_copy(dst, first[half][:].rearrange("p i (m t) -> p m i t", t=PACK))
+
         def quantize_weight(name, b, pieces=2):
             words = keep.tile([P, PASS], U32, name="words_%s%d" % (name, b), align_bytes=64)
             plane = keep.tile([P, PASS], U8, name="plane_%s%d" % (name, b), align_bytes=64)
@@ -146,22 +150,10 @@ def tile_list_meltab_mix_pow_kernel(
         def square_tile(b, j0, width):
             squares[b, j0] = keep.tile([P, 2, width // LINE, PACK, LINE], F32, name="squares%d_%d" % (b, j0))
 
-        def square_part(name, b, base, j0, width):
-            rows = slice((j0 - base) // LINE, (j0 - base + width) // LINE)
-            for t in range(PACK):
-                bank = sums.tile([P, PASS], F32, name="bank")
-                transform(bank[:, :width], name, b, t, j0, width)
-                nc.scalar.activation(
-                    squares[b, base][:, ("co", "si").index(name), rows, t, :],
-                    bank[:, :width].rearrange("p (c i) -> p c i", i=LINE),
-                    ACT.Square,
-                    scale=root[:, b * PACK + t : b * PACK + t + 1],
-                )
-
         by_frame = {}
 
-        def square_by_frame(name, jt):
-            w_words, w_plane = packed[name, 0]
+        def square_by_frame(name, b, jt):
+            w_words, w_plane = packed[name, b]
             cols = slice(jt * P, (jt + 1) * P)
             bank = sums.tile([P, PASS], F32, name="bank")
             nc.tensor.matmul_mx(
@@ -173,43 +165,52 @@ def tile_list_meltab_mix_pow_kernel(
                 start=True,
                 stop=True,
             )
-            by_frame[name, jt] = keep.tile([P, PASS], F32, name="by_frame_%s%d" % (name, jt))
-            nc.scalar.activation(by_frame[name, jt][:], bank[:], ACT.Square)
+            by_frame[name, b, jt] = keep.tile([P, PASS], F32, name="by_frame_%s%d_%d" % (name, b, jt))
+            nc.scalar.activation(by_frame[name, b, jt][:], bank[:], ACT.Square)
 
-        def turn_and_scale(jt):
+        def turn_and_scale(b, jt, width):
             bank = results.tile([P, PACK, P], F32, name="acc")
             for t in range(PACK):
                 for name in ("co", "si"):
                     nc.tensor.matmul(
                         bank[:, t, :],
-                        by_frame[name, jt][:, t * P : (t + 1) * P],
+                        by_frame[name, b, jt][:, t * P : (t + 1) * P],
                         identity[:],
                         start=name == "co",
                         stop=name == "si",
                         is_transpose=True,
                     )
-            j0 = jt * P - jt * P % LOW_WIDTH
-            if (0, j0) not in signed:
-                signed[0, j0] = keep.tile([P, LOW_WIDTH, PACK], BF16, name="signed0_%d" % j0, align_bytes=64)
+            j0 = jt * P - jt * P % width
+            if (b, j0) not in signed:
+                signed[b, j0] = keep.tile([P, width, PACK], BF16, name="signed%d_%d" % (b, j0), align_bytes=64)
             nc.vector.tensor_tensor(
-                signed[0, j0][:, jt * P - j0 : (jt + 1) * P - j0, :],
+                signed[b, j0][:, jt * P - j0 : (jt + 1) * P - j0, :],
                 bank[:].rearrange("p t j -> p j t"),
-                gain[:, 0].unsqueeze(1).to_broadcast([P, P, PACK]),
+                gain[:, b].unsqueeze(1).to_broadcast([P, P, PACK]),
                 ALU.mult,
             )
 
-        def square_both(b, j0, width):
-            square_tile(b, j0, width)
-            for t in range(PACK):
-                bank = sums.tile([P, PASS], F32, name="bank")
-                transform(bank[:, :width], "co", b, t, j0, width)
-                transform(bank[:, width : 2 * width], "si", b, t, j0, width)
-                nc.scalar.activation(
-                    squares[b, j0][:, :, :, t, :].rearrange("p s c i -> p (s c) i"),
-                    bank[:, : 2 * width].rearrange("p (c i) -> p c i", i=LINE),
-                    ACT.Square,
-                    scale=root[:, b * PACK + t : b * PACK + t + 1],
-                )
+        def square_slot(name, b, base, t):
+            bank = sums.tile([P, PASS], F32, name="bank")
+            transform(bank[:], name, b, t, base, PASS)
+            nc.scalar.activation(
+                squares[b, base][:, ("co", "si").index(name), :, t, :],
+                bank[:].rearrange("p (c i) -> p c i", i=LINE),
+                ACT.Square,
+                scale=root[:, b * PACK + t : b * PACK + t + 1],
+            )
+
+        def square_pair(b, j0, t):
+            width = PASS // 2
+            bank = sums.tile([P, PASS], F32, name="bank")
+            transform(bank[:, :width], "co", b, t, j0, width)
+            transform(bank[:, width:], "si", b, t, j0, width)
+            nc.scalar.activation(
+                squares[b, j0][:, :, :, t, :].rearrange("p s c i -> p (s c) i"),
+                bank[:].rearrange("p (c i) -> p c i", i=LINE),
+                ACT.Square,
+                scale=root[:, b * PACK + t : b * PACK + t + 1],
+            )
 
         unsigned = {}
         signed = {}
@@ -281,43 +282,69 @@ def tile_list_meltab_mix_pow_kernel(
             nc.sync.dma_start(out=out.rearrange("(a p) j -> p a j", p=P)[:, :, j0 : j0 + width], in_=staged[:])
 
         gather_scales(0, 1024)
-        cast_weight(nc.vector.tensor_copy, "co", 0, 0)
-        cast_weight(nc.vector.tensor_copy, "co", 0, 1)
-        quantize_weight("co", 0, 2)
+        cast_first(nc.scalar.copy, 0)
+        cast_first(nc.vector.tensor_copy, 1)
+        quantize_weight("co", 0)
         gather_words(0, 256)
         gather_words(256, 256)
         gather_words(512, 512)
-        for jt in range(LOW_WIDTH // P):
-            square_by_frame("co", jt)
+        for jt in range(4):
+            square_by_frame("co", 0, jt)
         square_tile(0, 512, 512)
-        square_part("co", 0, 512, 512, 512)
-        cast_weight(nc.vector.tensor_copy, "si", 0, 0)
-        cast_weight(nc.vector.tensor_copy, "si", 0, 1)
-        quantize_weight("si", 0)
-        for jt in range(LOW_WIDTH // P):
-            square_by_frame("si", jt)
-        cast_weight(nc.vector.tensor_copy, "co", 1, 0)
-        cast_weight(nc.vector.tensor_copy, "co", 1, 1)
-        quantize_weight("co", 1)
-        cast_weight(nc.vector.tensor_copy, "si", 1, 0)
-        cast_weight(nc.scalar.copy, "si", 1, 1)
-        square_part("si", 0, 512, 512, 512)
-        quantize_weight("si", 1)
-        for jt in range(LOW_WIDTH // P):
-            turn_and_scale(jt)
+        for t in range(PACK):
+            square_slot("co", 0, 512, t)
+        for name, b in (("si", 0), ("co", 1), ("si", 1)):
+            cast_weight(nc.vector.tensor_copy, name, b, 0)
+            cast_weight(nc.vector.tensor_copy, name, b, 1)
+            quantize_weight(name, b)
 
-        for step in range(len(UNITS) + 2):
-            if step < len(UNITS):
-                b, j0, width = UNITS[step]
-                if b == 1 and j0 % 256 == 0:
-                    square_both(b, j0, 256)
-                add(b, j0, width)
-            if step == 0:
-                quantize_power(0, 0, LOW_WIDTH)
-            if 1 <= step <= len(UNITS):
-                apply_sign(*UNITS[step - 1])
-            if step >= 2:
-                b, j0, width = UNITS[step - 2]
-                quantize_power(b, j0, width)
-                if b == 1:
-                    filter_bank(j0, width)
+        def low(jt):
+            square_by_frame("si", 0, jt)
+            turn_and_scale(0, jt, 256)
+
+        def high(jt):
+            square_by_frame("co", 1, jt)
+            square_by_frame("si", 1, jt)
+            turn_and_scale(1, jt, 128 if jt >= 2 else 256)
+
+        low(0)
+        square_slot("si", 0, 512, 0)
+        square_slot("si", 0, 512, 1)
+        low(1)
+        square_slot("si", 0, 512, 2)
+        square_slot("si", 0, 512, 3)
+        add(0, 512, 512)
+        low(2)
+        quantize_power(0, 0, 256)
+        apply_sign(0, 512, 512)
+        square_tile(1, 512, 256)
+        square_pair(1, 512, 0)
+        square_pair(1, 512, 1)
+        low(3)
+        quantize_power(0, 512, 512)
+        square_pair(1, 512, 2)
+        square_pair(1, 512, 3)
+        add(1, 512, 256)
+        quantize_power(0, 256, 256)
+        apply_sign(1, 512, 256)
+        high(0)
+        quantize_power(1, 512, 256)
+        square_tile(1, 768, 256)
+        square_pair(1, 768, 0)
+        filter_bank(512, 256)
+        high(1)
+        square_pair(1, 768, 1)
+        quantize_power(1, 0, 256)
+        square_pair(1, 768, 2)
+        square_pair(1, 768, 3)
+        filter_bank(0, 256)
+        add(1, 768, 256)
+        high(2)
+        apply_sign(1, 768, 256)
+        quantize_power(1, 256, 128)
+        quantize_power(1, 768, 256)
+        high(3)
+        filter_bank(256, 128)
+        filter_bank(768, 256)
+        quantize_power(1, 384, 128)
+        filter_bank(384, 128)

@@ -47,8 +47,8 @@ def tile_list_meltab_mix_pow_kernel(
         fb4 = keep.tile([P, N // 2], I32, name="fb4", align_bytes=64)
         gain = keep.tile([P, 2, PACK], F32, name="gain")
 
-        nc.vector.memset(table_plane[:], 0)
-        nc.vector.memset(fb_plane[:], 0)
+        nc.gpsimd.memset(table_plane[:], 0)
+        nc.gpsimd.memset(fb_plane[:], 0)
         weights = {"co": co, "si": si}
         raw = {}
 
@@ -60,14 +60,13 @@ def tile_list_meltab_mix_pow_kernel(
             )
 
         nc.sync.dma_start(offsets[:], offs)
-        nc.sync.dma_start(out=gain[:], in_=gn.rearrange("(b p t) -> p b t", b=2, t=PACK))
-        load_scale_rows(nc.sync, table_plane, tab_scales[0])
         co_rows = co.rearrange("(p i) f -> p i f", i=PACK)
-        first = []
-        for half in range(2):
-            first.append(keep.tile([P, PACK, PASS // 2], F32, name="raw_co0_%d" % half))
-            nc.sync.dma_start(out=first[half][:], in_=co_rows[:, :, half * 256 : (half + 1) * 256])
+        first = [keep.tile([P, PACK, PASS // 2], F32, name="raw_co0_%d" % half) for half in range(2)]
+        nc.sync.dma_start(out=first[0][:], in_=co_rows[:, :, : PASS // 2])
+        load_scale_rows(nc.sync, table_plane, tab_scales[0])
+        nc.sync.dma_start(out=first[1][:], in_=co_rows[:, :, PASS // 2 : PASS])
         nc.sync.dma_start(out=table[:], in_=tab_words[0].rearrange("p t i -> p (t i)").bitcast(I32))
+        nc.sync.dma_start(out=gain[:], in_=gn.rearrange("(b p t) -> p b t", b=2, t=PACK))
         load_weight("si", 0)
         load_weight("co", 1)
         load_weight("si", 1)
@@ -79,14 +78,18 @@ def tile_list_meltab_mix_pow_kernel(
         identity = keep.tile([P, P], F32, name="identity")
         make_identity(nc, identity[:])
         flat_gain = gain[:].rearrange("p b t -> p (b t)")
+        step = keep.tile([P, 2 * PACK], F32, name="step")
+        sign32 = keep.tile([P, 2 * PACK], F32, name="sign32")
         size = keep.tile([P, 2 * PACK], F32, name="size")
         half_power = keep.tile([P, 2 * PACK], F32, name="half_power")
         root = keep.tile([P, 2 * PACK], F32, name="root")
         sign = keep.tile([P, 2 * PACK], BF16, name="sign")
         nc.gpsimd.memset(half_power[:], 0.5)
-        nc.scalar.activation(size[:], flat_gain, ACT.Abs)
-        nc.scalar.activation(sign[:], flat_gain, ACT.Sign)
+        nc.gpsimd.tensor_scalar(step[:], flat_gain, 0.0, 2.0, ALU.is_ge, ALU.mult)
+        nc.gpsimd.tensor_scalar(sign32[:], step[:], 1.0, -1.0, ALU.mult, ALU.add)
+        nc.gpsimd.tensor_tensor(size[:], flat_gain, sign32[:], ALU.mult)
         nc.gpsimd.tensor_tensor(root[:], size[:], half_power[:], ALU.pow)
+        nc.gpsimd.tensor_scalar(sign[:], step[:], 1.0, -1.0, ALU.mult, ALU.add)
 
         frame_words = keep.tile([P, J], U32, name="frame_words", align_bytes=64)
         frame_plane = keep.tile([P, J], U8, name="frame_plane", align_bytes=64)
@@ -168,18 +171,21 @@ def tile_list_meltab_mix_pow_kernel(
             by_frame[name, b, jt] = keep.tile([P, PASS], F32, name="by_frame_%s%d_%d" % (name, b, jt))
             nc.scalar.activation(by_frame[name, b, jt][:], bank[:], ACT.Square)
 
-        def turn_and_scale(b, jt, width):
+        def turn_and_scale(b, jt, width, last=False):
             bank = results.tile([P, PACK, P], F32, name="acc")
-            for t in range(PACK):
-                for name in ("co", "si"):
-                    nc.tensor.matmul(
-                        bank[:, t, :],
-                        by_frame[name, b, jt][:, t * P : (t + 1) * P],
-                        identity[:],
-                        start=name == "co",
-                        stop=name == "si",
-                        is_transpose=True,
-                    )
+            if last:
+                order = [(name, t) for name in ("co", "si") for t in range(PACK)]
+            else:
+                order = [(name, t) for t in range(PACK) for name in ("co", "si")]
+            for name, t in order:
+                nc.tensor.matmul(
+                    bank[:, t, :],
+                    by_frame[name, b, jt][:, t * P : (t + 1) * P],
+                    identity[:],
+                    start=name == "co" and (t == 0 or not last),
+                    stop=name == "si" and (t == PACK - 1 or not last),
+                    is_transpose=True,
+                )
             j0 = jt * P - jt * P % width
             if (b, j0) not in signed:
                 signed[b, j0] = keep.tile([P, width, PACK], BF16, name="signed%d_%d" % (b, j0), align_bytes=64)
@@ -250,7 +256,7 @@ def tile_list_meltab_mix_pow_kernel(
         fb_bytes = fb_plane[:].bitcast(U8)
 
         def filter_bank(j0, width):
-            acc = results.tile([P, PASS], F32, name="acc")
+            acc = sums.tile([P, PASS], F32, name="bank")
             for nt in range(N // P):
                 for g0 in range(0, width, GROUP):
                     cols = slice(j0 + g0, j0 + g0 + GROUP)
@@ -283,7 +289,7 @@ def tile_list_meltab_mix_pow_kernel(
 
         gather_scales(0, 1024)
         cast_first(nc.scalar.copy, 0)
-        cast_first(nc.vector.tensor_copy, 1)
+        cast_first(nc.scalar.copy, 1)
         quantize_weight("co", 0)
         gather_words(0, 256)
         gather_words(256, 256)
@@ -298,6 +304,7 @@ def tile_list_meltab_mix_pow_kernel(
             cast_weight(nc.vector.tensor_copy, name, b, 1)
             quantize_weight(name, b)
 
+
         def low(jt):
             square_by_frame("si", 0, jt)
             turn_and_scale(0, jt, 256)
@@ -305,7 +312,7 @@ def tile_list_meltab_mix_pow_kernel(
         def high(jt):
             square_by_frame("co", 1, jt)
             square_by_frame("si", 1, jt)
-            turn_and_scale(1, jt, 128 if jt >= 2 else 256)
+            turn_and_scale(1, jt, 128 if jt >= 2 else 256, jt == 3)
 
         low(0)
         square_slot("si", 0, 512, 0)
@@ -331,20 +338,20 @@ def tile_list_meltab_mix_pow_kernel(
         quantize_power(1, 512, 256)
         square_tile(1, 768, 256)
         square_pair(1, 768, 0)
-        filter_bank(512, 256)
-        high(1)
         square_pair(1, 768, 1)
-        quantize_power(1, 0, 256)
+        high(1)
         square_pair(1, 768, 2)
+        quantize_power(1, 0, 256)
         square_pair(1, 768, 3)
-        filter_bank(0, 256)
         add(1, 768, 256)
         high(2)
         apply_sign(1, 768, 256)
         quantize_power(1, 256, 128)
         quantize_power(1, 768, 256)
         high(3)
-        filter_bank(256, 128)
-        filter_bank(768, 256)
         quantize_power(1, 384, 128)
+        filter_bank(512, 256)
+        filter_bank(0, 256)
+        filter_bank(768, 256)
+        filter_bank(256, 128)
         filter_bank(384, 128)

@@ -63,10 +63,10 @@ def tile_list_meltab_mix_pow_kernel(
         co_rows = co.rearrange("(p i) f -> p i f", i=PACK)
         first = [keep.tile([P, PACK, PASS // 2], F32, name="raw_co0_%d" % half) for half in range(2)]
         nc.sync.dma_start(out=first[0][:], in_=co_rows[:, :, : PASS // 2])
+        nc.sync.dma_start(out=gain[:], in_=gn.rearrange("(b p t) -> p b t", b=2, t=PACK))
         load_scale_rows(nc.sync, table_plane, tab_scales[0])
         nc.sync.dma_start(out=first[1][:], in_=co_rows[:, :, PASS // 2 : PASS])
         nc.sync.dma_start(out=table[:], in_=tab_words[0].rearrange("p t i -> p (t i)").bitcast(I32))
-        nc.sync.dma_start(out=gain[:], in_=gn.rearrange("(b p t) -> p b t", b=2, t=PACK))
         load_weight("si", 0)
         load_weight("co", 1)
         load_weight("si", 1)
@@ -78,18 +78,14 @@ def tile_list_meltab_mix_pow_kernel(
         identity = keep.tile([P, P], F32, name="identity")
         make_identity(nc, identity[:])
         flat_gain = gain[:].rearrange("p b t -> p (b t)")
-        step = keep.tile([P, 2 * PACK], F32, name="step")
-        sign32 = keep.tile([P, 2 * PACK], F32, name="sign32")
         size = keep.tile([P, 2 * PACK], F32, name="size")
         half_power = keep.tile([P, 2 * PACK], F32, name="half_power")
         root = keep.tile([P, 2 * PACK], F32, name="root")
         sign = keep.tile([P, 2 * PACK], BF16, name="sign")
         nc.gpsimd.memset(half_power[:], 0.5)
-        nc.gpsimd.tensor_scalar(step[:], flat_gain, 0.0, 2.0, ALU.is_ge, ALU.mult)
-        nc.gpsimd.tensor_scalar(sign32[:], step[:], 1.0, -1.0, ALU.mult, ALU.add)
-        nc.gpsimd.tensor_tensor(size[:], flat_gain, sign32[:], ALU.mult)
+        nc.scalar.activation(size[:], flat_gain, ACT.Abs)
+        nc.scalar.activation(sign[:], flat_gain, ACT.Sign)
         nc.gpsimd.tensor_tensor(root[:], size[:], half_power[:], ALU.pow)
-        nc.gpsimd.tensor_scalar(sign[:], step[:], 1.0, -1.0, ALU.mult, ALU.add)
 
         frame_words = keep.tile([P, J], U32, name="frame_words", align_bytes=64)
         frame_plane = keep.tile([P, J], U8, name="frame_plane", align_bytes=64)
@@ -297,8 +293,7 @@ def tile_list_meltab_mix_pow_kernel(
         for jt in range(4):
             square_by_frame("co", 0, jt)
         square_tile(0, 512, 512)
-        for t in range(PACK):
-            square_slot("co", 0, 512, t)
+        square_slot("co", 0, 512, 0)
         for name, b in (("si", 0), ("co", 1), ("si", 1)):
             cast_weight(nc.vector.tensor_copy, name, b, 0)
             cast_weight(nc.vector.tensor_copy, name, b, 1)
@@ -315,11 +310,11 @@ def tile_list_meltab_mix_pow_kernel(
             turn_and_scale(1, jt, 128 if jt >= 2 else 256, jt == 3)
 
         low(0)
-        square_slot("si", 0, 512, 0)
-        square_slot("si", 0, 512, 1)
+        for t in range(1, PACK):
+            square_slot("co", 0, 512, t)
         low(1)
-        square_slot("si", 0, 512, 2)
-        square_slot("si", 0, 512, 3)
+        for t in range(PACK):
+            square_slot("si", 0, 512, t)
         add(0, 512, 512)
         low(2)
         quantize_power(0, 0, 256)

@@ -36,8 +36,8 @@ def tile_list_meltab_mix_pow_kernel(
     nc = tc.nc
     with ExitStack() as ctx:
         keep = ctx.enter_context(tc.tile_pool(name="keep", bufs=1))
-        sums = ctx.enter_context(tc.psum_pool(name="sums", bufs=4))
-        results = ctx.enter_context(tc.psum_pool(name="results", bufs=4))
+        sums = ctx.enter_context(tc.psum_pool(name="sums", bufs=5))
+        results = ctx.enter_context(tc.psum_pool(name="results", bufs=3))
 
         offsets = keep.tile([P, J // 16], U16, name="offsets")
         table = keep.tile([P, T], I32, name="table", align_bytes=64)
@@ -67,9 +67,13 @@ def tile_list_meltab_mix_pow_kernel(
         load_scale_rows(nc.sync, table_plane, tab_scales[0])
         nc.sync.dma_start(out=first[1][:], in_=co_rows[:, :, PASS // 2 : PASS])
         nc.sync.dma_start(out=table[:], in_=tab_words[0].rearrange("p t i -> p (t i)").bitcast(I32))
-        load_weight("si", 0)
-        load_weight("co", 1)
-        load_weight("si", 1)
+        halves = {}
+        for name, b in (("si", 0), ("co", 1), ("si", 1)):
+            rows = weights[name].rearrange("(p i) f -> p i f", i=PACK)
+            for half in range(2):
+                halves[name, b, half] = keep.tile([P, PACK, 256], F32, name="raw_%s%d_%d" % (name, b, half))
+                f0 = b * PASS + half * 256
+                nc.sync.dma_start(out=halves[name, b, half][:], in_=rows[:, :, f0 : f0 + 256])
         nc.sync.dma_start(out=fb8[:], in_=fb8_words[0].rearrange("p n i -> p (n i)").bitcast(I32))
         nc.sync.dma_start(out=fb4[:], in_=fb4_words[0].bitcast(I32))
         load_scale_rows(nc.sync, fb_plane[:, : N // 4], fb8_scales[0])
@@ -118,6 +122,15 @@ def tile_list_meltab_mix_pow_kernel(
                 grouped["co", 0] = keep.tile([P, PACK, P, PACK], BF16, name="grouped_co0", align_bytes=64)
             dst = grouped["co", 0][:, :, half * 64 : (half + 1) * 64, :].rearrange("p t m i -> p m i t")
             engine_copy(dst, first[half][:].rearrange("p i (m t) -> p m i t", t=PACK))
+
+        def cast_half(name, b, half, slots):
+            if (name, b) not in grouped:
+                grouped[name, b] = keep.tile(
+                    [P, PACK, P, PACK], BF16, name="grouped_%s%d" % (name, b), align_bytes=64
+                )
+            dst = grouped[name, b][:, :, half * 64 : (half + 1) * 64, :].rearrange("p t m i -> p m i t")
+            src = halves[name, b, half][:].rearrange("p i (m t) -> p m i t", t=PACK)
+            nc.vector.tensor_copy(dst[:, :, :, slots], src[:, :, :, slots])
 
         def quantize_weight(name, b, pieces=2):
             words = keep.tile([P, PASS], U32, name="words_%s%d" % (name, b), align_bytes=64)
@@ -214,6 +227,19 @@ def tile_list_meltab_mix_pow_kernel(
                 scale=root[:, b * PACK + t : b * PACK + t + 1],
             )
 
+        def square_quad(b, j0, t0):
+            bank = sums.tile([P, 2, 2, P], F32, name="bank")
+            for t in range(2):
+                transform(bank[:, t, 0, :], "co", b, t0 + t, j0, P)
+                transform(bank[:, t, 1, :], "si", b, t0 + t, j0, P)
+            for t in range(2):
+                nc.scalar.activation(
+                    squares[b, j0][:, :, :, t0 + t, :].rearrange("p s c i -> p (s c) i"),
+                    bank[:, t].rearrange("p s (c i) -> p (s c) i", i=LINE),
+                    ACT.Square,
+                    scale=root[:, b * PACK + t0 + t : b * PACK + t0 + t + 1],
+                )
+
         unsigned = {}
         signed = {}
 
@@ -283,6 +309,31 @@ def tile_list_meltab_mix_pow_kernel(
                 nc.scalar.copy(flat, acc[:, : 2 * width])
             nc.sync.dma_start(out=out.rearrange("(a p) j -> p a j", p=P)[:, :, j0 : j0 + width], in_=staged[:])
 
+        def filter_wide(j0, nt):
+            acc = sums.tile([P, PASS], F32, name="bank")
+            cols = slice(j0, j0 + PASS)
+            nc.tensor.matmul_mx(
+                out=acc[:],
+                lhsT=fb8[:, nt * P : (nt + 1) * P].bitcast(FP8X4),
+                lhsT_scale=fb_bytes[:, nt * P : (nt + 1) * P],
+                rhs=power_words[0][:, cols].bitcast(FP8X4),
+                rhs_scale=power_plane[0][:, cols],
+                start=True,
+                stop=False,
+            )
+            nc.tensor.matmul_mx(
+                out=acc[:],
+                lhsT=fb4[:].bitcast(U8)[:, nt * 2 * P : (nt + 1) * 2 * P].bitcast(FP4X4),
+                lhsT_scale=fb_bytes[:, N + nt * P : N + (nt + 1) * P],
+                rhs=power_words[1][:, cols].bitcast(FP8X4),
+                rhs_scale=power_plane[1][:, cols],
+                start=False,
+                stop=True,
+            )
+            staged = keep.tile([P, PASS], F32, name="wide%d_%d" % (j0, nt))
+            nc.scalar.copy(staged[:], acc[:])
+            nc.sync.dma_start(out=out[nt * P : (nt + 1) * P, cols], in_=staged[:])
+
         gather_scales(0, 1024)
         cast_first(nc.scalar.copy, 0)
         cast_first(nc.scalar.copy, 1)
@@ -295,8 +346,9 @@ def tile_list_meltab_mix_pow_kernel(
         square_tile(0, 512, 512)
         square_slot("co", 0, 512, 0)
         for name, b in (("si", 0), ("co", 1), ("si", 1)):
-            cast_weight(nc.vector.tensor_copy, name, b, 0)
-            cast_weight(nc.vector.tensor_copy, name, b, 1)
+            cast_half(name, b, 0, slice(0, 4))
+            cast_half(name, b, 1, slice(0, 2))
+            cast_half(name, b, 1, slice(2, 4))
             quantize_weight(name, b)
 
 
@@ -343,10 +395,14 @@ def tile_list_meltab_mix_pow_kernel(
         apply_sign(1, 768, 256)
         quantize_power(1, 256, 128)
         quantize_power(1, 768, 256)
-        high(3)
+        square_tile(1, 384, 128)
+        for t in range(0, PACK, 2):
+            square_quad(1, 384, t)
+        add(1, 384, 128)
+        apply_sign(1, 384, 128)
         quantize_power(1, 384, 128)
-        filter_bank(512, 256)
         filter_bank(0, 256)
-        filter_bank(768, 256)
+        filter_wide(512, 0)
+        filter_wide(512, 1)
         filter_bank(256, 128)
         filter_bank(384, 128)

@@ -47,33 +47,26 @@ def tile_list_meltab_mix_pow_kernel(
         fb4 = keep.tile([P, N // 2], I32, name="fb4", align_bytes=64)
         gain = keep.tile([P, 2, PACK], F32, name="gain")
 
-        nc.gpsimd.memset(table_plane[:], 0)
+        nc.vector.memset(table_plane[:], 0)
         nc.gpsimd.memset(fb_plane[:], 0)
         weights = {"co": co, "si": si}
-        raw = {}
+        halves = {}
 
-        def load_weight(name, b):
-            raw[name, b] = keep.tile([P, PACK, PASS], F32, name="raw_%s%d" % (name, b))
-            nc.sync.dma_start(
-                out=raw[name, b][:],
-                in_=weights[name].rearrange("(p i) f -> p i f", i=PACK)[:, :, b * PASS : (b + 1) * PASS],
-            )
+        def load_half(name, b, half):
+            rows = weights[name].rearrange("(p i) f -> p i f", i=PACK)
+            halves[name, b, half] = keep.tile([P, PACK, 256], F32, name="raw_%s%d_%d" % (name, b, half))
+            f0 = b * PASS + half * 256
+            nc.sync.dma_start(out=halves[name, b, half][:], in_=rows[:, :, f0 : f0 + 256])
 
         nc.sync.dma_start(offsets[:], offs)
-        co_rows = co.rearrange("(p i) f -> p i f", i=PACK)
-        first = [keep.tile([P, PACK, PASS // 2], F32, name="raw_co0_%d" % half) for half in range(2)]
-        nc.sync.dma_start(out=first[0][:], in_=co_rows[:, :, : PASS // 2])
-        nc.sync.dma_start(out=gain[:], in_=gn.rearrange("(b p t) -> p b t", b=2, t=PACK))
+        load_half("co", 0, 0)
         load_scale_rows(nc.sync, table_plane, tab_scales[0])
-        nc.sync.dma_start(out=first[1][:], in_=co_rows[:, :, PASS // 2 : PASS])
+        load_half("co", 0, 1)
         nc.sync.dma_start(out=table[:], in_=tab_words[0].rearrange("p t i -> p (t i)").bitcast(I32))
-        halves = {}
+        nc.sync.dma_start(out=gain[:], in_=gn.rearrange("(b p t) -> p b t", b=2, t=PACK))
         for name, b in (("si", 0), ("co", 1), ("si", 1)):
-            rows = weights[name].rearrange("(p i) f -> p i f", i=PACK)
             for half in range(2):
-                halves[name, b, half] = keep.tile([P, PACK, 256], F32, name="raw_%s%d_%d" % (name, b, half))
-                f0 = b * PASS + half * 256
-                nc.sync.dma_start(out=halves[name, b, half][:], in_=rows[:, :, f0 : f0 + 256])
+                load_half(name, b, half)
         nc.sync.dma_start(out=fb8[:], in_=fb8_words[0].rearrange("p n i -> p (n i)").bitcast(I32))
         nc.sync.dma_start(out=fb4[:], in_=fb4_words[0].bitcast(I32))
         load_scale_rows(nc.sync, fb_plane[:, : N // 4], fb8_scales[0])
@@ -107,42 +100,32 @@ def tile_list_meltab_mix_pow_kernel(
         grouped = {}
         packed = {}
 
-        def cast_weight(engine_copy, name, b, half):
-            if (name, b) not in grouped:
+        for name in ("co", "si"):
+            for b in range(2):
                 grouped[name, b] = keep.tile(
-                    [P, PACK, P, PACK], BF16, name="grouped_%s%d" % (name, b), align_bytes=64
+                    [P, 2, 2, P, PACK], BF16, name="grouped_%s%d" % (name, b), align_bytes=64
                 )
-            slots = slice(2 * half, 2 * half + 2)
-            dst = grouped[name, b][:].rearrange("p t m i -> p m i t")
-            src = raw[name, b][:].rearrange("p i (m t) -> p m i t", t=PACK)
-            engine_copy(dst[:, :, :, slots], src[:, :, :, slots])
-
-        def cast_first(engine_copy, half):
-            if ("co", 0) not in grouped:
-                grouped["co", 0] = keep.tile([P, PACK, P, PACK], BF16, name="grouped_co0", align_bytes=64)
-            dst = grouped["co", 0][:, :, half * 64 : (half + 1) * 64, :].rearrange("p t m i -> p m i t")
-            engine_copy(dst, first[half][:].rearrange("p i (m t) -> p m i t", t=PACK))
-
-        def cast_half(name, b, half, slots):
-            if (name, b) not in grouped:
-                grouped[name, b] = keep.tile(
-                    [P, PACK, P, PACK], BF16, name="grouped_%s%d" % (name, b), align_bytes=64
+                packed[name, b] = (
+                    keep.tile([P, PASS], U32, name="words_%s%d" % (name, b), align_bytes=64),
+                    keep.tile([P, PASS], U8, name="plane_%s%d" % (name, b), align_bytes=64),
                 )
-            dst = grouped[name, b][:, :, half * 64 : (half + 1) * 64, :].rearrange("p t m i -> p m i t")
-            src = halves[name, b, half][:].rearrange("p i (m t) -> p m i t", t=PACK)
-            nc.vector.tensor_copy(dst[:, :, :, slots], src[:, :, :, slots])
 
-        def quantize_weight(name, b, pieces=2):
-            words = keep.tile([P, PASS], U32, name="words_%s%d" % (name, b), align_bytes=64)
-            plane = keep.tile([P, PASS], U8, name="plane_%s%d" % (name, b), align_bytes=64)
-            step = PACK // pieces
-            for t in range(0, PACK, step):
-                nc.vector.quantize_mx(
-                    out=words[:, t * P : (t + step) * P].bitcast(FP8X4),
-                    scales=plane[:, t * P : (t + step) * P],
-                    in_=grouped[name, b][:, t : t + step].rearrange("p t m i -> p (t m i)"),
-                )
-            packed[name, b] = (words, plane)
+        def cast(engine_copy, name, b, half, pair=None):
+            dst = grouped[name, b][:, :, :, half * 64 : (half + 1) * 64, :].rearrange("p u e m i -> p u m i e")
+            src = halves[name, b, half][:].rearrange("p i (m u e) -> p u m i e", u=2, e=2)
+            if pair is None:
+                engine_copy(dst, src)
+            else:
+                engine_copy(dst[:, pair], src[:, pair])
+
+        def quantize_weight(name, b, pair):
+            words, plane = packed[name, b]
+            cols = slice(pair * 2 * P, (pair + 1) * 2 * P)
+            nc.vector.quantize_mx(
+                out=words[:, cols].bitcast(FP8X4),
+                scales=plane[:, cols],
+                in_=grouped[name, b][:, pair].rearrange("p e m i -> p (e m i)"),
+            )
 
         def transform(bank_cols, name, b, t, j0, width):
             w_words, w_plane = packed[name, b]
@@ -335,74 +318,75 @@ def tile_list_meltab_mix_pow_kernel(
             nc.sync.dma_start(out=out[nt * P : (nt + 1) * P, cols], in_=staged[:])
 
         gather_scales(0, 1024)
-        cast_first(nc.scalar.copy, 0)
-        cast_first(nc.scalar.copy, 1)
-        quantize_weight("co", 0)
+        cast(nc.scalar.copy, "co", 0, 0)
+        cast(nc.scalar.copy, "co", 0, 1)
+        quantize_weight("co", 0, 0)
+        quantize_weight("co", 0, 1)
         gather_words(0, 256)
-        gather_words(256, 256)
         gather_words(512, 512)
-        for jt in range(4):
-            square_by_frame("co", 0, jt)
-        square_tile(0, 512, 512)
-        square_slot("co", 0, 512, 0)
+        gather_words(256, 256)
         for name, b in (("si", 0), ("co", 1), ("si", 1)):
-            cast_half(name, b, 0, slice(0, 4))
-            cast_half(name, b, 1, slice(0, 2))
-            cast_half(name, b, 1, slice(2, 4))
-            quantize_weight(name, b)
+            for half in range(2):
+                for pair in range(2):
+                    cast(nc.vector.tensor_copy, name, b, half, pair)
+            quantize_weight(name, b, 0)
+            quantize_weight(name, b, 1)
 
+        def turned(b, jt, width):
+            square_by_frame("co", b, jt)
+            square_by_frame("si", b, jt)
+            turn_and_scale(b, jt, width)
 
         def low(jt):
             square_by_frame("si", 0, jt)
             turn_and_scale(0, jt, 256)
 
-        def high(jt):
-            square_by_frame("co", 1, jt)
-            square_by_frame("si", 1, jt)
-            turn_and_scale(1, jt, 128 if jt >= 2 else 256, jt == 3)
-
-        low(0)
-        for t in range(1, PACK):
+        square_by_frame("co", 0, 0)
+        square_by_frame("co", 0, 1)
+        square_tile(0, 512, 512)
+        for t in range(PACK):
             square_slot("co", 0, 512, t)
-        low(1)
+        low(0)
         for t in range(PACK):
             square_slot("si", 0, 512, t)
-        add(0, 512, 512)
-        low(2)
+        add(0, 512, 256)
+        add(0, 768, 256)
+        low(1)
+        apply_sign(0, 512, 256)
+        apply_sign(0, 768, 256)
+        turned(0, 2, 256)
         quantize_power(0, 0, 256)
-        apply_sign(0, 512, 512)
+        quantize_power(0, 512, 256)
+        quantize_power(0, 768, 256)
         square_tile(1, 512, 256)
         square_pair(1, 512, 0)
         square_pair(1, 512, 1)
-        low(3)
-        quantize_power(0, 512, 512)
+        turned(0, 3, 256)
         square_pair(1, 512, 2)
         square_pair(1, 512, 3)
         add(1, 512, 256)
         quantize_power(0, 256, 256)
         apply_sign(1, 512, 256)
-        high(0)
+        turned(1, 0, 256)
         quantize_power(1, 512, 256)
         square_tile(1, 768, 256)
-        square_pair(1, 768, 0)
-        square_pair(1, 768, 1)
-        high(1)
-        square_pair(1, 768, 2)
-        quantize_power(1, 0, 256)
-        square_pair(1, 768, 3)
+        for t in range(PACK):
+            square_pair(1, 768, t)
         add(1, 768, 256)
-        high(2)
+        turned(1, 1, 256)
         apply_sign(1, 768, 256)
-        quantize_power(1, 256, 128)
+        quantize_power(1, 0, 256)
         quantize_power(1, 768, 256)
+        turned(1, 2, 128)
         square_tile(1, 384, 128)
         for t in range(0, PACK, 2):
             square_quad(1, 384, t)
         add(1, 384, 128)
+        quantize_power(1, 256, 128)
         apply_sign(1, 384, 128)
         quantize_power(1, 384, 128)
-        filter_bank(0, 256)
         filter_wide(512, 0)
         filter_wide(512, 1)
+        filter_bank(0, 256)
         filter_bank(256, 128)
         filter_bank(384, 128)

@@ -22,7 +22,7 @@ PACK = 4
 PASS = P * PACK
 LINE = 4
 GROUP = 128
-VECTOR_OUTS = {384}
+VECTOR_OUTS = {896}
 
 
 def load_scale_rows(queue, plane, rows):
@@ -47,26 +47,37 @@ def tile_list_meltab_mix_pow_kernel(
         fb4 = keep.tile([P, N // 2], I32, name="fb4", align_bytes=64)
         gain = keep.tile([P, 2, PACK], F32, name="gain")
 
-        nc.vector.memset(table_plane[:], 0)
+        nc.gpsimd.memset(table_plane[:], 0)
         nc.gpsimd.memset(fb_plane[:], 0)
         weights = {"co": co, "si": si}
         halves = {}
 
-        def load_half(name, b, half):
+        def load_columns(name, b, half, width, tag=None):
             rows = weights[name].rearrange("(p i) f -> p i f", i=PACK)
-            halves[name, b, half] = keep.tile([P, PACK, 256], F32, name="raw_%s%d_%d" % (name, b, half))
+            label = "raw_%s%d_%d" % (name, b, half)
+            tile = keep.tile([P, PACK, width], F32, name=label, tag=tag or label, align_bytes=64)
             f0 = b * PASS + half * 256
-            nc.sync.dma_start(out=halves[name, b, half][:], in_=rows[:, :, f0 : f0 + 256])
+            nc.sync.dma_start(out=tile[:], in_=rows[:, :, f0 : f0 + width])
+            return tile
+
+        def load_halves(name, b):
+            for half in range(2):
+                halves[name, b, half] = load_columns(name, b, half, 256)
+
+        whole = {}
+
+        def load_band(name, b, tag=None):
+            whole[name, b] = load_columns(name, b, 0, PASS, tag)
 
         nc.sync.dma_start(offsets[:], offs)
-        load_half("co", 0, 0)
-        load_scale_rows(nc.sync, table_plane, tab_scales[0])
-        load_half("co", 0, 1)
-        nc.sync.dma_start(out=table[:], in_=tab_words[0].rearrange("p t i -> p (t i)").bitcast(I32))
+        halves["co", 0, 0] = load_columns("co", 0, 0, 256)
         nc.sync.dma_start(out=gain[:], in_=gn.rearrange("(b p t) -> p b t", b=2, t=PACK))
-        for name, b in (("si", 0), ("co", 1), ("si", 1)):
-            for half in range(2):
-                load_half(name, b, half)
+        load_scale_rows(nc.sync, table_plane, tab_scales[0])
+        halves["co", 0, 1] = load_columns("co", 0, 1, 256)
+        nc.sync.dma_start(out=table[:], in_=tab_words[0].rearrange("p t i -> p (t i)").bitcast(I32))
+        load_band("si", 0, "si0_then_frames")
+        load_band("co", 1)
+        load_band("si", 1)
         nc.sync.dma_start(out=fb8[:], in_=fb8_words[0].rearrange("p n i -> p (n i)").bitcast(I32))
         nc.sync.dma_start(out=fb4[:], in_=fb4_words[0].bitcast(I32))
         load_scale_rows(nc.sync, fb_plane[:, : N // 4], fb8_scales[0])
@@ -84,18 +95,22 @@ def tile_list_meltab_mix_pow_kernel(
         nc.scalar.activation(sign[:], flat_gain, ACT.Sign)
         nc.gpsimd.tensor_tensor(root[:], size[:], half_power[:], ALU.pow)
 
-        frame_words = keep.tile([P, J], U32, name="frame_words", align_bytes=64)
         frame_plane = keep.tile([P, J], U8, name="frame_plane", align_bytes=64)
+        gathered = {}
 
-        def gather(dst, window, j0, width):
+        def gather_words(j0, width, tag=None):
+            label = "frame_words%d" % j0
+            gathered[j0] = keep.tile([P, width], U32, name=label, tag=tag or label, align_bytes=64)
             picks = offsets[:, j0 // 16 : (j0 + width) // 16]
-            nc.vector.tensor_copy(dst[:, j0 : j0 + width], window.indirect(picks))
+            nc.vector.tensor_copy(gathered[j0][:], table[:].bitcast(U32).indirect(picks))
 
-        def gather_words(j0, width):
-            gather(frame_words, table[:].bitcast(U32), j0, width)
+        def frame_words(cols):
+            j0 = max(start for start in gathered if start <= cols.start)
+            return gathered[j0][:, cols.start - j0 : cols.stop - j0].bitcast(FP8X4)
 
         def gather_scales(j0, width):
-            gather(frame_plane, table_plane[:].bitcast(U8), j0, width)
+            picks = offsets[:, j0 // 16 : (j0 + width) // 16]
+            nc.vector.tensor_copy(frame_plane[:, j0 : j0 + width], table_plane[:].bitcast(U8).indirect(picks))
 
         grouped = {}
         packed = {}
@@ -118,6 +133,18 @@ def tile_list_meltab_mix_pow_kernel(
             else:
                 engine_copy(dst[:, pair], src[:, pair])
 
+        def cast_half(engine_copy, name, b, half):
+            engine_copy(
+                grouped[name, b][:, :, :, half * 64 : (half + 1) * 64, :].rearrange("p u e m i -> p m i (u e)"),
+                halves[name, b, half][:].rearrange("p i (m t) -> p m i t", t=PACK),
+            )
+
+        def cast_band(engine_copy, name, b, pair):
+            engine_copy(
+                grouped[name, b][:, pair].rearrange("p e m i -> p m i e"),
+                whole[name, b][:].rearrange("p i (m u e) -> p u m i e", u=2, e=2)[:, pair],
+            )
+
         def quantize_weight(name, b, pair):
             words, plane = packed[name, b]
             cols = slice(pair * 2 * P, (pair + 1) * 2 * P)
@@ -134,7 +161,7 @@ def tile_list_meltab_mix_pow_kernel(
                 out=bank_cols,
                 lhsT=w_words[:, t * P : (t + 1) * P].bitcast(FP8X4),
                 lhsT_scale=w_plane[:, t * P : (t + 1) * P],
-                rhs=frame_words[:, cols].bitcast(FP8X4),
+                rhs=frame_words(cols),
                 rhs_scale=frame_plane[:, cols],
                 start=True,
                 stop=True,
@@ -153,7 +180,7 @@ def tile_list_meltab_mix_pow_kernel(
             bank = sums.tile([P, PASS], F32, name="bank")
             nc.tensor.matmul_mx(
                 out=bank[:],
-                lhsT=frame_words[:, cols].bitcast(FP8X4),
+                lhsT=frame_words(cols),
                 lhsT_scale=frame_plane[:, cols],
                 rhs=w_words[:].bitcast(FP8X4),
                 rhs_scale=w_plane[:],
@@ -163,21 +190,18 @@ def tile_list_meltab_mix_pow_kernel(
             by_frame[name, b, jt] = keep.tile([P, PASS], F32, name="by_frame_%s%d_%d" % (name, b, jt))
             nc.scalar.activation(by_frame[name, b, jt][:], bank[:], ACT.Square)
 
-        def turn_and_scale(b, jt, width, last=False):
+        def turn_and_scale(b, jt, width):
             bank = results.tile([P, PACK, P], F32, name="acc")
-            if last:
-                order = [(name, t) for name in ("co", "si") for t in range(PACK)]
-            else:
-                order = [(name, t) for t in range(PACK) for name in ("co", "si")]
-            for name, t in order:
-                nc.tensor.matmul(
-                    bank[:, t, :],
-                    by_frame[name, b, jt][:, t * P : (t + 1) * P],
-                    identity[:],
-                    start=name == "co" and (t == 0 or not last),
-                    stop=name == "si" and (t == PACK - 1 or not last),
-                    is_transpose=True,
-                )
+            for t in range(PACK):
+                for name in ("si", "co"):
+                    nc.tensor.matmul(
+                        bank[:, t, :],
+                        by_frame[name, b, jt][:, t * P : (t + 1) * P],
+                        identity[:],
+                        start=name == "si",
+                        stop=name == "co",
+                        is_transpose=True,
+                    )
             j0 = jt * P - jt * P % width
             if (b, j0) not in signed:
                 signed[b, j0] = keep.tile([P, width, PACK], BF16, name="signed%d_%d" % (b, j0), align_bytes=64)
@@ -209,6 +233,20 @@ def tile_list_meltab_mix_pow_kernel(
                 ACT.Square,
                 scale=root[:, b * PACK + t : b * PACK + t + 1],
             )
+
+        def square_duo(name, b, base, j0, t0):
+            width = PASS // 2
+            bank = sums.tile([P, 2, width], F32, name="bank")
+            rows = slice((j0 - base) // LINE, (j0 - base + width) // LINE)
+            for t in range(2):
+                transform(bank[:, t, :], name, b, t0 + t, j0, width)
+            for t in range(2):
+                nc.scalar.activation(
+                    squares[b, base][:, ("co", "si").index(name), rows, t0 + t, :],
+                    bank[:, t].rearrange("p (c i) -> p c i", i=LINE),
+                    ACT.Square,
+                    scale=root[:, b * PACK + t0 + t : b * PACK + t0 + t + 1],
+                )
 
         def square_quad(b, j0, t0):
             bank = sums.tile([P, 2, 2, P], F32, name="bank")
@@ -318,75 +356,90 @@ def tile_list_meltab_mix_pow_kernel(
             nc.sync.dma_start(out=out[nt * P : (nt + 1) * P, cols], in_=staged[:])
 
         gather_scales(0, 1024)
-        cast(nc.scalar.copy, "co", 0, 0)
-        cast(nc.scalar.copy, "co", 0, 1)
+        cast_half(nc.scalar.copy, "co", 0, 0)
+        cast_half(nc.scalar.copy, "co", 0, 1)
         quantize_weight("co", 0, 0)
         quantize_weight("co", 0, 1)
         gather_words(0, 256)
         gather_words(512, 512)
-        gather_words(256, 256)
-        for name, b in (("si", 0), ("co", 1), ("si", 1)):
-            for half in range(2):
-                for pair in range(2):
-                    cast(nc.vector.tensor_copy, name, b, half, pair)
-            quantize_weight(name, b, 0)
-            quantize_weight(name, b, 1)
-
-        def turned(b, jt, width):
-            square_by_frame("co", b, jt)
-            square_by_frame("si", b, jt)
-            turn_and_scale(b, jt, width)
-
-        def low(jt):
-            square_by_frame("si", 0, jt)
-            turn_and_scale(0, jt, 256)
+        for pair in range(2):
+            cast_band(nc.vector.tensor_copy, "si", 0, pair)
+        for pair in range(2):
+            quantize_weight("si", 0, pair)
+        gather_words(256, 256, "si0_then_frames")
+        for pair in range(2):
+            cast_band(nc.vector.tensor_copy, "co", 1, pair)
+        for pair in range(2):
+            quantize_weight("co", 1, pair)
 
         square_by_frame("co", 0, 0)
         square_by_frame("co", 0, 1)
         square_tile(0, 512, 512)
+        square_tile(1, 512, 256)
+        square_tile(1, 768, 128)
+        square_tile(1, 896, 128)
         for t in range(PACK):
             square_slot("co", 0, 512, t)
-        low(0)
-        for t in range(PACK):
-            square_slot("si", 0, 512, t)
+        cast_band(nc.vector.tensor_copy, "si", 1, 0)
+        cast_band(nc.vector.tensor_copy, "si", 1, 1)
+        quantize_weight("si", 1, 0)
+        quantize_weight("si", 1, 1)
+        square_duo("si", 0, 512, 512, 0)
+        square_duo("si", 0, 512, 512, 2)
+        square_by_frame("si", 0, 0)
+        square_duo("si", 0, 512, 768, 0)
+        square_duo("si", 0, 512, 768, 2)
+        square_by_frame("si", 0, 1)
+        square_by_frame("co", 0, 2)
+        turn_and_scale(0, 0, 256)
+        square_by_frame("co", 0, 3)
+        square_by_frame("si", 0, 2)
+        square_by_frame("co", 1, 0)
+        turn_and_scale(0, 1, 256)
+        square_by_frame("co", 1, 1)
+        square_by_frame("si", 0, 3)
+        square_pair(1, 512, 0)
+        turn_and_scale(0, 2, 256)
+        square_pair(1, 512, 1)
+        square_by_frame("si", 1, 0)
+        square_pair(1, 512, 2)
+        turn_and_scale(0, 3, 256)
+        square_pair(1, 512, 3)
+        square_by_frame("si", 1, 1)
+        square_by_frame("co", 1, 2)
+        turn_and_scale(1, 0, 256)
+        square_by_frame("co", 1, 3)
+        square_by_frame("si", 1, 2)
+        square_by_frame("si", 1, 3)
+        turn_and_scale(1, 1, 256)
+        square_quad(1, 768, 0)
+        square_quad(1, 768, 2)
+        square_quad(1, 896, 0)
+        turn_and_scale(1, 2, 128)
+        square_quad(1, 896, 2)
+        turn_and_scale(1, 3, 128)
+
         add(0, 512, 256)
         add(0, 768, 256)
-        low(1)
         apply_sign(0, 512, 256)
         apply_sign(0, 768, 256)
-        turned(0, 2, 256)
-        quantize_power(0, 0, 256)
-        quantize_power(0, 512, 256)
-        quantize_power(0, 768, 256)
-        square_tile(1, 512, 256)
-        square_pair(1, 512, 0)
-        square_pair(1, 512, 1)
-        turned(0, 3, 256)
-        square_pair(1, 512, 2)
-        square_pair(1, 512, 3)
+        for j0 in (512, 768, 0, 256):
+            quantize_power(0, j0, 256)
         add(1, 512, 256)
-        quantize_power(0, 256, 256)
         apply_sign(1, 512, 256)
-        turned(1, 0, 256)
-        quantize_power(1, 512, 256)
-        square_tile(1, 768, 256)
-        for t in range(PACK):
-            square_pair(1, 768, t)
-        add(1, 768, 256)
-        turned(1, 1, 256)
-        apply_sign(1, 768, 256)
         quantize_power(1, 0, 256)
-        quantize_power(1, 768, 256)
-        turned(1, 2, 128)
-        square_tile(1, 384, 128)
-        for t in range(0, PACK, 2):
-            square_quad(1, 384, t)
-        add(1, 384, 128)
+        quantize_power(1, 512, 256)
         quantize_power(1, 256, 128)
-        apply_sign(1, 384, 128)
+        add(1, 768, 128)
         quantize_power(1, 384, 128)
-        filter_wide(512, 0)
-        filter_wide(512, 1)
+        apply_sign(1, 768, 128)
+        add(1, 896, 128)
+        quantize_power(1, 768, 128)
+        apply_sign(1, 896, 128)
+        quantize_power(1, 896, 128)
+        filter_bank(512, 256)
         filter_bank(0, 256)
         filter_bank(256, 128)
         filter_bank(384, 128)
+        filter_bank(768, 128)
+        filter_bank(896, 128)

@@ -22,7 +22,6 @@ PACK = 4
 PASS = P * PACK
 LINE = 4
 GROUP = 128
-VECTOR_OUTS = {896}
 
 
 def load_scale_rows(queue, plane, rows):
@@ -70,8 +69,8 @@ def tile_list_meltab_mix_pow_kernel(
             whole[name, b] = load_columns(name, b, 0, PASS, tag)
 
         nc.sync.dma_start(offsets[:], offs)
-        halves["co", 0, 0] = load_columns("co", 0, 0, 256)
         nc.sync.dma_start(out=gain[:], in_=gn.rearrange("(b p t) -> p b t", b=2, t=PACK))
+        halves["co", 0, 0] = load_columns("co", 0, 0, 256)
         load_scale_rows(nc.sync, table_plane, tab_scales[0])
         halves["co", 0, 1] = load_columns("co", 0, 1, 256)
         nc.sync.dma_start(out=table[:], in_=tab_words[0].rearrange("p t i -> p (t i)").bitcast(I32))
@@ -139,10 +138,10 @@ def tile_list_meltab_mix_pow_kernel(
                 halves[name, b, half][:].rearrange("p i (m t) -> p m i t", t=PACK),
             )
 
-        def cast_band(engine_copy, name, b, pair):
+        def cast_band(engine_copy, name, b, pair, rows=slice(0, P)):
             engine_copy(
-                grouped[name, b][:, pair].rearrange("p e m i -> p m i e"),
-                whole[name, b][:].rearrange("p i (m u e) -> p u m i e", u=2, e=2)[:, pair],
+                grouped[name, b][:, pair].rearrange("p e m i -> p m i e")[:, rows],
+                whole[name, b][:].rearrange("p i (m u e) -> p u m i e", u=2, e=2)[:, pair, rows],
             )
 
         def quantize_weight(name, b, pair):
@@ -190,27 +189,39 @@ def tile_list_meltab_mix_pow_kernel(
             by_frame[name, b, jt] = keep.tile([P, PASS], F32, name="by_frame_%s%d_%d" % (name, b, jt))
             nc.scalar.activation(by_frame[name, b, jt][:], bank[:], ACT.Square)
 
-        def turn_and_scale(b, jt, width):
-            bank = results.tile([P, PACK, P], F32, name="acc")
-            for t in range(PACK):
-                for name in ("si", "co"):
-                    nc.tensor.matmul(
-                        bank[:, t, :],
-                        by_frame[name, b, jt][:, t * P : (t + 1) * P],
-                        identity[:],
-                        start=name == "si",
-                        stop=name == "co",
-                        is_transpose=True,
-                    )
+        turning = {}
+
+        def turn(names, b, jt, opens, closes):
+            if opens:
+                turning[b, jt] = results.tile([P, PACK, P], F32, name="acc")
+            steps = [(name, t) for name in names for t in range(PACK)]
+            for name, t in steps:
+                nc.tensor.matmul(
+                    turning[b, jt][:, t, :],
+                    by_frame[name, b, jt][:, t * P : (t + 1) * P],
+                    identity[:],
+                    start=opens and (name, t) == steps[0],
+                    stop=closes and (name, t) == steps[-1],
+                    is_transpose=True,
+                )
+
+        def scale_turned(b, jt, width):
             j0 = jt * P - jt * P % width
             if (b, j0) not in signed:
                 signed[b, j0] = keep.tile([P, width, PACK], BF16, name="signed%d_%d" % (b, j0), align_bytes=64)
             nc.vector.tensor_tensor(
                 signed[b, j0][:, jt * P - j0 : (jt + 1) * P - j0, :],
-                bank[:].rearrange("p t j -> p j t"),
+                turning[b, jt][:].rearrange("p t j -> p j t"),
                 gain[:, b].unsqueeze(1).to_broadcast([P, P, PACK]),
                 ALU.mult,
             )
+
+        def turn_and_scale(b, jt, width):
+            if (b, jt) in turning:
+                turn(("si",), b, jt, False, True)
+            else:
+                turn(("si", "co"), b, jt, True, True)
+            scale_turned(b, jt, width)
 
         def square_slot(name, b, base, t):
             bank = sums.tile([P, PASS], F32, name="bank")
@@ -264,17 +275,21 @@ def tile_list_meltab_mix_pow_kernel(
         unsigned = {}
         signed = {}
 
-        def add(b, j0, width):
-            tile = keep.tile([P, width, PACK], BF16, name="unsigned%d_%d" % (b, j0), align_bytes=64)
+        def add(b, j0, width, whole_width=None):
+            whole_width = whole_width or width
+            first = j0 - j0 % whole_width
+            if (b, first) not in unsigned:
+                unsigned[b, first] = keep.tile(
+                    [P, whole_width, PACK], BF16, name="unsigned%d_%d" % (b, first), align_bytes=64
+                )
             base = max(start for (half, start) in squares if half == b and start <= j0)
             rows = slice((j0 - base) // LINE, (j0 - base + width) // LINE)
             nc.vector.tensor_tensor(
-                tile[:].rearrange("p (c i) t -> p c t i", i=LINE),
+                unsigned[b, first][:, j0 - first : j0 - first + width].rearrange("p (c i) t -> p c t i", i=LINE),
                 squares[b, base][:, 0, rows],
                 squares[b, base][:, 1, rows],
                 ALU.add,
             )
-            unsigned[b, j0] = tile
 
         def apply_sign(b, j0, width):
             tile = keep.tile([P, width, PACK], BF16, name="signed%d_%d" % (b, j0), align_bytes=64)
@@ -298,62 +313,53 @@ def tile_list_meltab_mix_pow_kernel(
 
         fb_bytes = fb_plane[:].bitcast(U8)
 
-        def filter_bank(j0, width):
-            acc = sums.tile([P, PASS], F32, name="bank")
-            for nt in range(N // P):
-                for g0 in range(0, width, GROUP):
-                    cols = slice(j0 + g0, j0 + g0 + GROUP)
-                    dst = acc[:, nt * width + g0 : nt * width + g0 + GROUP]
-                    nc.tensor.matmul_mx(
-                        out=dst,
-                        lhsT=fb8[:, nt * P : (nt + 1) * P].bitcast(FP8X4),
-                        lhsT_scale=fb_bytes[:, nt * P : (nt + 1) * P],
-                        rhs=power_words[0][:, cols].bitcast(FP8X4),
-                        rhs_scale=power_plane[0][:, cols],
-                        start=True,
-                        stop=False,
-                    )
-                    nc.tensor.matmul_mx(
-                        out=dst,
-                        lhsT=fb4[:].bitcast(U8)[:, nt * 2 * P : (nt + 1) * 2 * P].bitcast(FP4X4),
-                        lhsT_scale=fb_bytes[:, N + nt * P : N + (nt + 1) * P],
-                        rhs=power_words[1][:, cols].bitcast(FP8X4),
-                        rhs_scale=power_plane[1][:, cols],
-                        start=False,
-                        stop=True,
-                    )
-            staged = keep.tile([P, N // P, width], F32, name="staged%d" % j0)
-            flat = staged[:].rearrange("p a j -> p (a j)")
-            if j0 in VECTOR_OUTS:
-                nc.vector.tensor_copy(flat, acc[:, : 2 * width])
+        def filter_pass(dst, b, nt, cols, start, stop):
+            if b == 0:
+                codes = fb8[:, nt * P : (nt + 1) * P].bitcast(FP8X4)
             else:
-                nc.scalar.copy(flat, acc[:, : 2 * width])
+                codes = fb4[:].bitcast(U8)[:, nt * 2 * P : (nt + 1) * 2 * P].bitcast(FP4X4)
+            nc.tensor.matmul_mx(
+                out=dst,
+                lhsT=codes,
+                lhsT_scale=fb_bytes[:, b * N + nt * P : b * N + (nt + 1) * P],
+                rhs=power_words[b][:, cols].bitcast(FP8X4),
+                rhs_scale=power_plane[b][:, cols],
+                start=start,
+                stop=stop,
+            )
+
+        filtered = {}
+
+        def filter_block(j0, width):
+            acc = sums.tile([P, N // P, width], F32, name="bank")
+            steps = [(b, g0, nt) for b in range(2) for g0 in range(0, width, GROUP) for nt in range(N // P)]
+            for step in steps:
+                b, g0, nt = step
+                cols = slice(j0 + g0, j0 + g0 + GROUP)
+                filter_pass(acc[:, nt, g0 : g0 + GROUP], b, nt, cols, step == steps[0], step == steps[-1])
+            filtered[j0] = (acc, width)
+
+        def store_block(j0):
+            acc, width = filtered[j0]
+            staged = keep.tile([P, N // P, width], F32, name="staged%d" % j0)
+            nc.scalar.copy(staged[:], acc[:])
             nc.sync.dma_start(out=out.rearrange("(a p) j -> p a j", p=P)[:, :, j0 : j0 + width], in_=staged[:])
 
-        def filter_wide(j0, nt):
-            acc = sums.tile([P, PASS], F32, name="bank")
-            cols = slice(j0, j0 + PASS)
-            nc.tensor.matmul_mx(
-                out=acc[:],
-                lhsT=fb8[:, nt * P : (nt + 1) * P].bitcast(FP8X4),
-                lhsT_scale=fb_bytes[:, nt * P : (nt + 1) * P],
-                rhs=power_words[0][:, cols].bitcast(FP8X4),
-                rhs_scale=power_plane[0][:, cols],
-                start=True,
-                stop=False,
-            )
-            nc.tensor.matmul_mx(
-                out=acc[:],
-                lhsT=fb4[:].bitcast(U8)[:, nt * 2 * P : (nt + 1) * 2 * P].bitcast(FP4X4),
-                lhsT_scale=fb_bytes[:, N + nt * P : N + (nt + 1) * P],
-                rhs=power_words[1][:, cols].bitcast(FP8X4),
-                rhs_scale=power_plane[1][:, cols],
-                start=False,
-                stop=True,
-            )
-            staged = keep.tile([P, PASS], F32, name="wide%d_%d" % (j0, nt))
-            nc.scalar.copy(staged[:], acc[:])
-            nc.sync.dma_start(out=out[nt * P : (nt + 1) * P, cols], in_=staged[:])
+        def filter_bank(j0, width):
+            filter_block(j0, width)
+            store_block(j0)
+
+        def filter_last(j0):
+            cols = slice(j0, j0 + GROUP)
+            accs = [results.tile([P, GROUP], F32, name="acc") for nt in range(N // P)]
+            for b in range(2):
+                for nt in range(N // P):
+                    filter_pass(accs[nt][:], b, nt, cols, b == 0, b == 1)
+            for nt, (engine_copy, queue) in enumerate(((nc.scalar.copy, nc.scalar), (nc.vector.tensor_copy, nc.sync))):
+                staged = keep.tile([P, GROUP], F32, name="last%d" % nt)
+                engine_copy(staged[:], accs[nt][:])
+                queue.dma_start(out=out[nt * P : (nt + 1) * P, cols], in_=staged[:])
+
 
         gather_scales(0, 1024)
         cast_half(nc.scalar.copy, "co", 0, 0)
@@ -380,6 +386,8 @@ def tile_list_meltab_mix_pow_kernel(
         square_tile(1, 896, 128)
         for t in range(PACK):
             square_slot("co", 0, 512, t)
+        for jt in range(2):
+            turn(("co",), 0, jt, True, False)
         cast_band(nc.vector.tensor_copy, "si", 1, 0)
         cast_band(nc.vector.tensor_copy, "si", 1, 1)
         quantize_weight("si", 1, 0)
@@ -391,19 +399,19 @@ def tile_list_meltab_mix_pow_kernel(
         square_duo("si", 0, 512, 768, 2)
         square_by_frame("si", 0, 1)
         square_by_frame("co", 0, 2)
-        turn_and_scale(0, 0, 256)
+        turn_and_scale(0, 0, 512)
         square_by_frame("co", 0, 3)
         square_by_frame("si", 0, 2)
         square_by_frame("co", 1, 0)
-        turn_and_scale(0, 1, 256)
+        turn_and_scale(0, 1, 512)
         square_by_frame("co", 1, 1)
         square_by_frame("si", 0, 3)
         square_pair(1, 512, 0)
-        turn_and_scale(0, 2, 256)
+        turn_and_scale(0, 2, 512)
         square_pair(1, 512, 1)
         square_by_frame("si", 1, 0)
         square_pair(1, 512, 2)
-        turn_and_scale(0, 3, 256)
+        turn_and_scale(0, 3, 512)
         square_pair(1, 512, 3)
         square_by_frame("si", 1, 1)
         square_by_frame("co", 1, 2)
@@ -419,27 +427,26 @@ def tile_list_meltab_mix_pow_kernel(
         square_quad(1, 896, 2)
         turn_and_scale(1, 3, 128)
 
-        add(0, 512, 256)
-        add(0, 768, 256)
-        apply_sign(0, 512, 256)
-        apply_sign(0, 768, 256)
-        for j0 in (512, 768, 0, 256):
-            quantize_power(0, j0, 256)
+        add(0, 512, 256, 512)
+        add(0, 768, 256, 512)
+        apply_sign(0, 512, 512)
+        quantize_power(0, 0, 512)
+        quantize_power(0, 512, 512)
         add(1, 512, 256)
         apply_sign(1, 512, 256)
         quantize_power(1, 0, 256)
         quantize_power(1, 512, 256)
-        quantize_power(1, 256, 128)
         add(1, 768, 128)
-        quantize_power(1, 384, 128)
         apply_sign(1, 768, 128)
-        add(1, 896, 128)
+        quantize_power(1, 256, 128)
         quantize_power(1, 768, 128)
+        add(1, 896, 128)
+        quantize_power(1, 384, 128)
         apply_sign(1, 896, 128)
         quantize_power(1, 896, 128)
         filter_bank(512, 256)
         filter_bank(0, 256)
         filter_bank(256, 128)
-        filter_bank(384, 128)
         filter_bank(768, 128)
-        filter_bank(896, 128)
+        filter_bank(384, 128)
+        filter_last(896)

@@ -21,7 +21,8 @@ P = 128
 PACK = 4
 PASS = P * PACK
 LINE = 4
-GROUP = 128
+GROUP = 256
+SUM_BANKS = 5
 
 
 def load_scale_rows(queue, plane, rows):
@@ -35,7 +36,7 @@ def tile_list_meltab_mix_pow_kernel(
     nc = tc.nc
     with ExitStack() as ctx:
         keep = ctx.enter_context(tc.tile_pool(name="keep", bufs=1))
-        sums = ctx.enter_context(tc.psum_pool(name="sums", bufs=5))
+        sums = ctx.enter_context(tc.psum_pool(name="sums", bufs=1))
         results = ctx.enter_context(tc.psum_pool(name="results", bufs=3))
 
         offsets = keep.tile([P, J // 16], U16, name="offsets")
@@ -153,6 +154,12 @@ def tile_list_meltab_mix_pow_kernel(
                 in_=grouped[name, b][:, pair].rearrange("p e m i -> p (e m i)"),
             )
 
+        taken = []
+
+        def next_bank(shape):
+            taken.append(shape)
+            return sums.tile(shape, F32, name="bank%d" % (len(taken) % SUM_BANKS))
+
         def transform(bank_cols, name, b, t, j0, width):
             w_words, w_plane = packed[name, b]
             cols = slice(j0, j0 + width)
@@ -176,7 +183,7 @@ def tile_list_meltab_mix_pow_kernel(
         def square_by_frame(name, b, jt):
             w_words, w_plane = packed[name, b]
             cols = slice(jt * P, (jt + 1) * P)
-            bank = sums.tile([P, PASS], F32, name="bank")
+            bank = next_bank([P, PASS])
             nc.tensor.matmul_mx(
                 out=bank[:],
                 lhsT=frame_words(cols),
@@ -224,7 +231,7 @@ def tile_list_meltab_mix_pow_kernel(
             scale_turned(b, jt, width)
 
         def square_slot(name, b, base, t):
-            bank = sums.tile([P, PASS], F32, name="bank")
+            bank = next_bank([P, PASS])
             transform(bank[:], name, b, t, base, PASS)
             nc.scalar.activation(
                 squares[b, base][:, ("co", "si").index(name), :, t, :],
@@ -235,7 +242,7 @@ def tile_list_meltab_mix_pow_kernel(
 
         def square_pair(b, j0, t):
             width = PASS // 2
-            bank = sums.tile([P, PASS], F32, name="bank")
+            bank = next_bank([P, PASS])
             transform(bank[:, :width], "co", b, t, j0, width)
             transform(bank[:, width:], "si", b, t, j0, width)
             nc.scalar.activation(
@@ -247,7 +254,7 @@ def tile_list_meltab_mix_pow_kernel(
 
         def square_duo(name, b, base, j0, t0):
             width = PASS // 2
-            bank = sums.tile([P, 2, width], F32, name="bank")
+            bank = next_bank([P, 2, width])
             rows = slice((j0 - base) // LINE, (j0 - base + width) // LINE)
             for t in range(2):
                 transform(bank[:, t, :], name, b, t0 + t, j0, width)
@@ -260,7 +267,7 @@ def tile_list_meltab_mix_pow_kernel(
                 )
 
         def square_quad(b, j0, t0):
-            bank = sums.tile([P, 2, 2, P], F32, name="bank")
+            bank = next_bank([P, 2, 2, P])
             for t in range(2):
                 transform(bank[:, t, 0, :], "co", b, t0 + t, j0, P)
                 transform(bank[:, t, 1, :], "si", b, t0 + t, j0, P)
@@ -331,32 +338,32 @@ def tile_list_meltab_mix_pow_kernel(
         filtered = {}
 
         def filter_block(j0, width):
-            acc = sums.tile([P, N // P, width], F32, name="bank")
-            steps = [(b, g0, nt) for b in range(2) for g0 in range(0, width, GROUP) for nt in range(N // P)]
+            acc = next_bank([P, N // P, width])
+            steps = [(b, g0, nt) for b in range(2) for g0 in range(0, width, min(GROUP, width)) for nt in range(N // P)]
             for step in steps:
                 b, g0, nt = step
-                cols = slice(j0 + g0, j0 + g0 + GROUP)
-                filter_pass(acc[:, nt, g0 : g0 + GROUP], b, nt, cols, step == steps[0], step == steps[-1])
+                cols = slice(j0 + g0, j0 + g0 + min(GROUP, width))
+                filter_pass(acc[:, nt, g0 : g0 + min(GROUP, width)], b, nt, cols, step == steps[0], step == steps[-1])
             filtered[j0] = (acc, width)
 
-        def store_block(j0):
+        def store_block(j0, engine_copy):
             acc, width = filtered[j0]
             staged = keep.tile([P, N // P, width], F32, name="staged%d" % j0)
-            nc.scalar.copy(staged[:], acc[:])
+            engine_copy(staged[:], acc[:])
             nc.sync.dma_start(out=out.rearrange("(a p) j -> p a j", p=P)[:, :, j0 : j0 + width], in_=staged[:])
 
-        def filter_bank(j0, width):
+        def filter_bank(j0, width, engine_copy=nc.scalar.copy):
             filter_block(j0, width)
-            store_block(j0)
+            store_block(j0, engine_copy)
 
         def filter_last(j0):
-            cols = slice(j0, j0 + GROUP)
-            accs = [results.tile([P, GROUP], F32, name="acc") for nt in range(N // P)]
+            cols = slice(j0, j0 + P)
+            accs = [results.tile([P, P], F32, name="acc") for nt in range(N // P)]
             for b in range(2):
                 for nt in range(N // P):
                     filter_pass(accs[nt][:], b, nt, cols, b == 0, b == 1)
-            for nt, (engine_copy, queue) in enumerate(((nc.scalar.copy, nc.scalar), (nc.vector.tensor_copy, nc.sync))):
-                staged = keep.tile([P, GROUP], F32, name="last%d" % nt)
+            for nt, (engine_copy, queue) in enumerate(((nc.scalar.copy, nc.sync), (nc.vector.tensor_copy, nc.sync))):
+                staged = keep.tile([P, P], F32, name="last%d" % nt)
                 engine_copy(staged[:], accs[nt][:])
                 queue.dma_start(out=out[nt * P : (nt + 1) * P, cols], in_=staged[:])
 
@@ -366,7 +373,8 @@ def tile_list_meltab_mix_pow_kernel(
         cast_half(nc.scalar.copy, "co", 0, 1)
         quantize_weight("co", 0, 0)
         quantize_weight("co", 0, 1)
-        gather_words(0, 256)
+        gather_words(0, 128)
+        gather_words(128, 128)
         gather_words(512, 512)
         for pair in range(2):
             cast_band(nc.vector.tensor_copy, "si", 0, pair)
@@ -378,75 +386,73 @@ def tile_list_meltab_mix_pow_kernel(
         for pair in range(2):
             quantize_weight("co", 1, pair)
 
-        square_by_frame("co", 0, 0)
-        square_by_frame("co", 0, 1)
         square_tile(0, 512, 512)
         square_tile(1, 512, 256)
-        square_tile(1, 768, 128)
         square_tile(1, 896, 128)
+        for jt in range(2):
+            square_by_frame("co", 0, jt)
         for t in range(PACK):
             square_slot("co", 0, 512, t)
-        for jt in range(2):
-            turn(("co",), 0, jt, True, False)
-        cast_band(nc.vector.tensor_copy, "si", 1, 0)
-        cast_band(nc.vector.tensor_copy, "si", 1, 1)
-        quantize_weight("si", 1, 0)
-        quantize_weight("si", 1, 1)
         square_duo("si", 0, 512, 512, 0)
         square_duo("si", 0, 512, 512, 2)
+        for jt in range(2):
+            turn(("co",), 0, jt, True, False)
+        for pair in range(2):
+            cast_band(nc.vector.tensor_copy, "si", 1, pair)
+        for pair in range(2):
+            quantize_weight("si", 1, pair)
         square_by_frame("si", 0, 0)
-        square_duo("si", 0, 512, 768, 0)
-        square_duo("si", 0, 512, 768, 2)
         square_by_frame("si", 0, 1)
         square_by_frame("co", 0, 2)
-        turn_and_scale(0, 0, 512)
-        square_by_frame("co", 0, 3)
         square_by_frame("si", 0, 2)
-        square_by_frame("co", 1, 0)
+        square_duo("si", 0, 512, 768, 0)
+        square_duo("si", 0, 512, 768, 2)
+        turn_and_scale(0, 0, 512)
         turn_and_scale(0, 1, 512)
-        square_by_frame("co", 1, 1)
+        square_by_frame("co", 0, 3)
         square_by_frame("si", 0, 3)
-        square_pair(1, 512, 0)
         turn_and_scale(0, 2, 512)
-        square_pair(1, 512, 1)
+        square_by_frame("co", 1, 0)
         square_by_frame("si", 1, 0)
-        square_pair(1, 512, 2)
+        square_pair(1, 512, 0)
+        square_by_frame("co", 1, 1)
         turn_and_scale(0, 3, 512)
-        square_pair(1, 512, 3)
         square_by_frame("si", 1, 1)
-        square_by_frame("co", 1, 2)
+        square_pair(1, 512, 1)
         turn_and_scale(1, 0, 256)
-        square_by_frame("co", 1, 3)
+        square_by_frame("co", 1, 2)
         square_by_frame("si", 1, 2)
-        square_by_frame("si", 1, 3)
+        square_pair(1, 512, 2)
         turn_and_scale(1, 1, 256)
-        square_quad(1, 768, 0)
-        square_quad(1, 768, 2)
-        square_quad(1, 896, 0)
+        square_pair(1, 512, 3)
+        square_by_frame("co", 1, 3)
+        square_by_frame("si", 1, 3)
         turn_and_scale(1, 2, 128)
+        square_by_frame("co", 1, 6)
+        square_by_frame("si", 1, 6)
+        square_quad(1, 896, 0)
         square_quad(1, 896, 2)
         turn_and_scale(1, 3, 128)
+        turn_and_scale(1, 6, 128)
 
         add(0, 512, 256, 512)
         add(0, 768, 256, 512)
         apply_sign(0, 512, 512)
         quantize_power(0, 0, 512)
         quantize_power(0, 512, 512)
-        add(1, 512, 256)
-        apply_sign(1, 512, 256)
         quantize_power(1, 0, 256)
-        quantize_power(1, 512, 256)
-        add(1, 768, 128)
-        apply_sign(1, 768, 128)
+        add(1, 512, 256)
         quantize_power(1, 256, 128)
-        quantize_power(1, 768, 128)
-        add(1, 896, 128)
+        apply_sign(1, 512, 256)
+        quantize_power(1, 512, 256)
         quantize_power(1, 384, 128)
+        add(1, 896, 128)
+        quantize_power(1, 768, 128)
         apply_sign(1, 896, 128)
         quantize_power(1, 896, 128)
-        filter_bank(512, 256)
         filter_bank(0, 256)
         filter_bank(256, 128)
-        filter_bank(768, 128)
+        filter_bank(512, 256)
         filter_bank(384, 128)
+        filter_bank(768, 128, nc.vector.tensor_copy)
         filter_last(896)

@@ -212,23 +212,25 @@ def tile_list_meltab_mix_pow_kernel(
                     is_transpose=True,
                 )
 
-        def scale_turned(b, jt, width):
-            j0 = jt * P - jt * P % width
-            if (b, j0) not in signed:
-                signed[b, j0] = keep.tile([P, width, PACK], BF16, name="signed%d_%d" % (b, j0), align_bytes=64)
+        power = [keep.tile([P, J, PACK], BF16, name="power%d" % b, align_bytes=64) for b in range(2)]
+
+        def scale_turned(b, jt):
             nc.vector.tensor_tensor(
-                signed[b, j0][:, jt * P - j0 : (jt + 1) * P - j0, :],
+                power[b][:, jt * P : (jt + 1) * P, :],
                 turning[b, jt][:].rearrange("p t j -> p j t"),
                 gain[:, b].unsqueeze(1).to_broadcast([P, P, PACK]),
                 ALU.mult,
             )
 
-        def turn_and_scale(b, jt, width):
+        def close_turn(b, jt):
             if (b, jt) in turning:
                 turn(("si",), b, jt, False, True)
             else:
                 turn(("si", "co"), b, jt, True, True)
-            scale_turned(b, jt, width)
+
+        def turn_and_scale(b, jt):
+            close_turn(b, jt)
+            scale_turned(b, jt)
 
         def square_slot(name, b, base, t):
             bank = next_bank([P, PASS])
@@ -280,7 +282,6 @@ def tile_list_meltab_mix_pow_kernel(
                 )
 
         unsigned = {}
-        signed = {}
 
         def add(b, j0, width, whole_width=None):
             whole_width = whole_width or width
@@ -299,14 +300,12 @@ def tile_list_meltab_mix_pow_kernel(
             )
 
         def apply_sign(b, j0, width):
-            tile = keep.tile([P, width, PACK], BF16, name="signed%d_%d" % (b, j0), align_bytes=64)
             nc.vector.tensor_tensor(
-                tile[:],
+                power[b][:, j0 : j0 + width, :],
                 unsigned[b, j0][:],
                 sign[:, b * PACK : (b + 1) * PACK].unsqueeze(1).to_broadcast([P, width, PACK]),
                 ALU.mult,
             )
-            signed[b, j0] = tile
 
         power_words = [keep.tile([P, J], U32, name="power_words%d" % b, align_bytes=64) for b in range(2)]
         power_plane = [keep.tile([P, J], U8, name="power_plane%d" % b, align_bytes=64) for b in range(2)]
@@ -315,7 +314,7 @@ def tile_list_meltab_mix_pow_kernel(
             nc.vector.quantize_mx(
                 out=power_words[b][:, j0 : j0 + width].bitcast(FP8X4),
                 scales=power_plane[b][:, j0 : j0 + width],
-                in_=signed[b, j0][:].rearrange("p j t -> p (j t)"),
+                in_=power[b][:, j0 : j0 + width, :].rearrange("p j t -> p (j t)"),
             )
 
         fb_bytes = fb_plane[:].bitcast(U8)
@@ -373,86 +372,93 @@ def tile_list_meltab_mix_pow_kernel(
         cast_half(nc.scalar.copy, "co", 0, 1)
         quantize_weight("co", 0, 0)
         quantize_weight("co", 0, 1)
+        spare = results.tile([P, PASS], F32, name="acc")
+        for repeat in range(4):
+            nc.tensor.matmul_mx(
+                out=spare[:, : 2 * P],
+                lhsT=packed["co", 0][0][:, :P].bitcast(FP8X4),
+                lhsT_scale=packed["co", 0][1][:, :P],
+                rhs=packed["co", 0][0][:, : 2 * P].bitcast(FP8X4),
+                rhs_scale=packed["co", 0][1][:, : 2 * P],
+                start=True,
+                stop=True,
+            )
         gather_words(0, 128)
         gather_words(128, 128)
-        gather_words(512, 512)
+        gather_words(256, 256)
+        gather_words(512, 256)
         for pair in range(2):
             cast_band(nc.vector.tensor_copy, "si", 0, pair)
         for pair in range(2):
             quantize_weight("si", 0, pair)
-        gather_words(256, 256, "si0_then_frames")
+        gather_words(768, 256, "si0_then_frames")
         for pair in range(2):
             cast_band(nc.vector.tensor_copy, "co", 1, pair)
         for pair in range(2):
             quantize_weight("co", 1, pair)
 
-        square_tile(0, 512, 512)
+        square_tile(0, 512, 256)
+        square_tile(0, 768, 256)
         square_tile(1, 512, 256)
         square_tile(1, 896, 128)
-        for jt in range(2):
+        for jt in range(4):
             square_by_frame("co", 0, jt)
-        for t in range(PACK):
-            square_slot("co", 0, 512, t)
-        square_duo("si", 0, 512, 512, 0)
-        square_duo("si", 0, 512, 512, 2)
-        for jt in range(2):
+        for name in ("co", "si"):
+            for t0 in (0, 2):
+                square_duo(name, 0, 512, 512, t0)
+        for jt in range(3):
             turn(("co",), 0, jt, True, False)
         for pair in range(2):
             cast_band(nc.vector.tensor_copy, "si", 1, pair)
         for pair in range(2):
             quantize_weight("si", 1, pair)
-        square_by_frame("si", 0, 0)
-        square_by_frame("si", 0, 1)
-        square_by_frame("co", 0, 2)
-        square_by_frame("si", 0, 2)
-        square_duo("si", 0, 512, 768, 0)
-        square_duo("si", 0, 512, 768, 2)
-        turn_and_scale(0, 0, 512)
-        turn_and_scale(0, 1, 512)
-        square_by_frame("co", 0, 3)
-        square_by_frame("si", 0, 3)
-        turn_and_scale(0, 2, 512)
+        for jt in range(4):
+            square_by_frame("si", 0, jt)
+        for t in range(PACK):
+            square_pair(0, 768, t)
+            turn_and_scale(0, t)
         square_by_frame("co", 1, 0)
         square_by_frame("si", 1, 0)
         square_pair(1, 512, 0)
         square_by_frame("co", 1, 1)
-        turn_and_scale(0, 3, 512)
         square_by_frame("si", 1, 1)
         square_pair(1, 512, 1)
-        turn_and_scale(1, 0, 256)
+        turn_and_scale(1, 0)
         square_by_frame("co", 1, 2)
         square_by_frame("si", 1, 2)
         square_pair(1, 512, 2)
-        turn_and_scale(1, 1, 256)
+        turn_and_scale(1, 1)
         square_pair(1, 512, 3)
         square_by_frame("co", 1, 3)
         square_by_frame("si", 1, 3)
-        turn_and_scale(1, 2, 128)
+        close_turn(1, 2)
         square_by_frame("co", 1, 6)
         square_by_frame("si", 1, 6)
         square_quad(1, 896, 0)
         square_quad(1, 896, 2)
-        turn_and_scale(1, 3, 128)
-        turn_and_scale(1, 6, 128)
+        close_turn(1, 3)
+        close_turn(1, 6)
 
         add(0, 512, 256, 512)
         add(0, 768, 256, 512)
         apply_sign(0, 512, 512)
-        quantize_power(0, 0, 512)
-        quantize_power(0, 512, 512)
+        quantize_power(0, 0, 1024)
         quantize_power(1, 0, 256)
         add(1, 512, 256)
-        quantize_power(1, 256, 128)
         apply_sign(1, 512, 256)
+        scale_turned(1, 2)
         quantize_power(1, 512, 256)
-        quantize_power(1, 384, 128)
+        quantize_power(1, 256, 128)
+        scale_turned(1, 3)
         add(1, 896, 128)
-        quantize_power(1, 768, 128)
+        quantize_power(1, 384, 128)
+        scale_turned(1, 6)
         apply_sign(1, 896, 128)
+        quantize_power(1, 768, 128)
         quantize_power(1, 896, 128)
         filter_bank(0, 256)
-        filter_bank(256, 128)
         filter_bank(512, 256)
+        filter_bank(256, 128)
         filter_bank(384, 128)
         filter_bank(768, 128, nc.vector.tensor_copy)
         filter_last(896)

@@ -372,17 +372,6 @@ def tile_list_meltab_mix_pow_kernel(
         cast_half(nc.scalar.copy, "co", 0, 1)
         quantize_weight("co", 0, 0)
         quantize_weight("co", 0, 1)
-        spare = results.tile([P, PASS], F32, name="acc")
-        for repeat in range(4):
-            nc.tensor.matmul_mx(
-                out=spare[:, : 2 * P],
-                lhsT=packed["co", 0][0][:, :P].bitcast(FP8X4),
-                lhsT_scale=packed["co", 0][1][:, :P],
-                rhs=packed["co", 0][0][:, : 2 * P].bitcast(FP8X4),
-                rhs_scale=packed["co", 0][1][:, : 2 * P],
-                start=True,
-                stop=True,
-            )
         gather_words(0, 128)
         gather_words(128, 128)
         gather_words(256, 256)

@@ -37,7 +37,7 @@ def tile_list_meltab_mix_pow_kernel(
     with ExitStack() as ctx:
         keep = ctx.enter_context(tc.tile_pool(name="keep", bufs=1))
         sums = ctx.enter_context(tc.psum_pool(name="sums", bufs=1))
-        results = ctx.enter_context(tc.psum_pool(name="results", bufs=3))
+        results = ctx.enter_context(tc.psum_pool(name="results", bufs=1))
 
         offsets = keep.tile([P, J // 16], U16, name="offsets")
         table = keep.tile([P, T], I32, name="table", align_bytes=64)
@@ -196,12 +196,35 @@ def tile_list_meltab_mix_pow_kernel(
             by_frame[name, b, jt] = keep.tile([P, PASS], F32, name="by_frame_%s%d_%d" % (name, b, jt))
             nc.scalar.activation(by_frame[name, b, jt][:], bank[:], ACT.Square)
 
+        def square_two_tiles(name, b, jt, pair):
+            w_words, w_plane = packed[name, b]
+            slots = slice(pair * 2 * P, (pair + 1) * 2 * P)
+            bank = next_bank([P, 2, 2 * P])
+            if pair == 0:
+                both = keep.tile([P, 2, PASS], F32, name="two_tiles_%s%d_%d" % (name, b, jt))
+                two_tiles[name, b, jt] = both
+                for a in range(2):
+                    by_frame[name, b, jt + a] = both[:, a]
+            for a in range(2):
+                cols = slice((jt + a) * P, (jt + a + 1) * P)
+                nc.tensor.matmul_mx(
+                    out=bank[:, a, :],
+                    lhsT=frame_words(cols),
+                    lhsT_scale=frame_plane[:, cols],
+                    rhs=w_words[:, slots].bitcast(FP8X4),
+                    rhs_scale=w_plane[:, slots],
+                    start=True,
+                    stop=True,
+                )
+            nc.scalar.activation(two_tiles[name, b, jt][:, :, slots], bank[:], ACT.Square)
+
+        two_tiles = {}
         turning = {}
 
         def turn(names, b, jt, opens, closes):
             if opens:
-                turning[b, jt] = results.tile([P, PACK, P], F32, name="acc")
-            steps = [(name, t) for name in names for t in range(PACK)]
+                turning[b, jt] = results.tile([P, PACK, P], F32, name="acc%d" % (len(turning) % 3))
+            steps = [(name, t) for name in names for t in reversed(range(PACK))]
             for name, t in steps:
                 nc.tensor.matmul(
                     turning[b, jt][:, t, :],
@@ -256,7 +279,10 @@ def tile_list_meltab_mix_pow_kernel(
 
         def square_duo(name, b, base, j0, t0):
             width = PASS // 2
-            bank = next_bank([P, 2, width])
+            if (name, t0) == ("si", 2):
+                bank = results.tile([P, 2, width], F32, name="acc2")
+            else:
+                bank = next_bank([P, 2, width])
             rows = slice((j0 - base) // LINE, (j0 - base + width) // LINE)
             for t in range(2):
                 transform(bank[:, t, :], name, b, t0 + t, j0, width)
@@ -357,7 +383,7 @@ def tile_list_meltab_mix_pow_kernel(
 
         def filter_last(j0):
             cols = slice(j0, j0 + P)
-            accs = [results.tile([P, P], F32, name="acc") for nt in range(N // P)]
+            accs = [results.tile([P, P], F32, name="acc%d" % nt) for nt in range(N // P)]
             for b in range(2):
                 for nt in range(N // P):
                     filter_pass(accs[nt][:], b, nt, cols, b == 0, b == 1)
@@ -401,11 +427,15 @@ def tile_list_meltab_mix_pow_kernel(
             cast_band(nc.vector.tensor_copy, "si", 1, pair)
         for pair in range(2):
             quantize_weight("si", 1, pair)
-        for jt in range(4):
+        for pair in range(2):
+            square_two_tiles("si", 0, 0, pair)
+        for jt in (2, 3):
             square_by_frame("si", 0, jt)
         for t in range(PACK):
             square_pair(0, 768, t)
-            turn_and_scale(0, t)
+            if t >= 1:
+                for jt in ((0, 1), (2,), (3,))[t - 1]:
+                    turn_and_scale(0, jt)
         square_by_frame("co", 1, 0)
         square_by_frame("si", 1, 0)
         square_pair(1, 512, 0)

@@ -20,9 +20,11 @@ ALU = mybir.AluOpType
 P = 128
 PACK = 4
 PASS = P * PACK
+HALF = PASS // 2
 LINE = 4
-GROUP = 256
 SUM_BANKS = 5
+TURN_BANKS = 3
+OWN = 128
 
 
 def load_scale_rows(queue, plane, rows):
@@ -37,122 +39,114 @@ def tile_list_meltab_mix_pow_kernel(
     with ExitStack() as ctx:
         keep = ctx.enter_context(tc.tile_pool(name="keep", bufs=1))
         sums = ctx.enter_context(tc.psum_pool(name="sums", bufs=1))
-        results = ctx.enter_context(tc.psum_pool(name="results", bufs=1))
+        turns = ctx.enter_context(tc.psum_pool(name="turns", bufs=1))
+
+        def sbuf(shape, dtype, name, tag=None):
+            return keep.tile(shape, dtype, name=name, tag=tag or name, align_bytes=64)
 
         offsets = keep.tile([P, J // 16], U16, name="offsets")
-        table = keep.tile([P, T], I32, name="table", align_bytes=64)
-        table_plane = keep.tile([P, T // 4], I32, name="table_plane", align_bytes=64)
-        fb_plane = keep.tile([P, 2 * N // 4], I32, name="fb_plane", align_bytes=64)
-        fb8 = keep.tile([P, N], I32, name="fb8", align_bytes=64)
-        fb4 = keep.tile([P, N // 2], I32, name="fb4", align_bytes=64)
-        gain = keep.tile([P, 2, PACK], F32, name="gain")
+        table = sbuf([P, T], I32, "table")
+        table_plane = sbuf([P, T // 4], I32, "table_plane")
+        fb_plane = sbuf([P, 2 * N // 4], I32, "fb_plane")
+        fb8 = sbuf([P, N], I32, "fb8")
+        fb4 = sbuf([P, N // 2], I32, "fb4")
+        gain = sbuf([P, 2, PACK], F32, "gain")
 
         nc.gpsimd.memset(table_plane[:], 0)
         nc.gpsimd.memset(fb_plane[:], 0)
-        weights = {"co": co, "si": si}
-        halves = {}
 
-        def load_columns(name, b, half, width, tag=None):
-            rows = weights[name].rearrange("(p i) f -> p i f", i=PACK)
-            label = "raw_%s%d_%d" % (name, b, half)
-            tile = keep.tile([P, PACK, width], F32, name=label, tag=tag or label, align_bytes=64)
-            f0 = b * PASS + half * 256
-            nc.sync.dma_start(out=tile[:], in_=rows[:, :, f0 : f0 + width])
+        def load_columns(matrix, f0, width, name):
+            tile = sbuf([P, PACK, width], F32, name)
+            nc.sync.dma_start(out=tile[:], in_=matrix.rearrange("(p i) f -> p i f", i=PACK)[:, :, f0 : f0 + width])
             return tile
-
-        def load_halves(name, b):
-            for half in range(2):
-                halves[name, b, half] = load_columns(name, b, half, 256)
-
-        whole = {}
-
-        def load_band(name, b, tag=None):
-            whole[name, b] = load_columns(name, b, 0, PASS, tag)
 
         nc.sync.dma_start(offsets[:], offs)
         nc.sync.dma_start(out=gain[:], in_=gn.rearrange("(b p t) -> p b t", b=2, t=PACK))
-        halves["co", 0, 0] = load_columns("co", 0, 0, 256)
+        raw_half = [load_columns(co, 0, HALF, "raw_half0")]
         load_scale_rows(nc.sync, table_plane, tab_scales[0])
-        halves["co", 0, 1] = load_columns("co", 0, 1, 256)
+        raw_half.append(load_columns(co, HALF, HALF, "raw_half1"))
         nc.sync.dma_start(out=table[:], in_=tab_words[0].rearrange("p t i -> p (t i)").bitcast(I32))
-        load_band("si", 0, "si0_then_frames")
-        load_band("co", 1)
-        load_band("si", 1)
+        raw = {
+            ("si", 0): load_columns(si, 0, PASS, "raw_si0"),
+            ("co", 1): load_columns(co, PASS, PASS, "raw_co1"),
+            ("si", 1): load_columns(si, PASS, PASS, "raw_si1"),
+        }
         nc.sync.dma_start(out=fb8[:], in_=fb8_words[0].rearrange("p n i -> p (n i)").bitcast(I32))
         nc.sync.dma_start(out=fb4[:], in_=fb4_words[0].bitcast(I32))
         load_scale_rows(nc.sync, fb_plane[:, : N // 4], fb8_scales[0])
         load_scale_rows(nc.sync, fb_plane[:, N // 4 :], fb4_scales[0])
 
-        identity = keep.tile([P, P], F32, name="identity")
+        identity = sbuf([P, P], F32, "identity")
         make_identity(nc, identity[:])
-        flat_gain = gain[:].rearrange("p b t -> p (b t)")
-        size = keep.tile([P, 2 * PACK], F32, name="size")
-        half_power = keep.tile([P, 2 * PACK], F32, name="half_power")
-        root = keep.tile([P, 2 * PACK], F32, name="root")
-        sign = keep.tile([P, 2 * PACK], BF16, name="sign")
+        size = sbuf([P, 2 * PACK], F32, "size")
+        twice = sbuf([P, 2 * PACK], F32, "twice")
+        half_power = sbuf([P, 2 * PACK], F32, "half_power")
+        root = sbuf([P, 2 * PACK], F32, "root")
+        sign = sbuf([P, 2 * PACK], BF16, "sign")
         nc.gpsimd.memset(half_power[:], 0.5)
-        nc.scalar.activation(size[:], flat_gain, ACT.Abs)
-        nc.scalar.activation(sign[:], flat_gain, ACT.Sign)
+        flat_gain = gain[:].rearrange("p b t -> p (b t)")
+        nc.gpsimd.tensor_scalar(twice[:], flat_gain, 0.0, 2.0, ALU.is_ge, ALU.mult)
+        nc.gpsimd.tensor_scalar(sign[:], twice[:], 1.0, -1.0, ALU.mult, ALU.add)
+        nc.gpsimd.tensor_tensor(size[:], flat_gain, sign[:], ALU.mult)
         nc.gpsimd.tensor_tensor(root[:], size[:], half_power[:], ALU.pow)
 
-        frame_plane = keep.tile([P, J], U8, name="frame_plane", align_bytes=64)
-        gathered = {}
+        frame_planes = {}
+        frame_words = {}
 
-        def gather_words(j0, width, tag=None):
-            label = "frame_words%d" % j0
-            gathered[j0] = keep.tile([P, width], U32, name=label, tag=tag or label, align_bytes=64)
-            picks = offsets[:, j0 // 16 : (j0 + width) // 16]
-            nc.vector.tensor_copy(gathered[j0][:], table[:].bitcast(U32).indirect(picks))
+        def piece(tiles, j0, width):
+            start = max(first for first in tiles if first <= j0)
+            return tiles[start][:, j0 - start : j0 - start + width]
 
-        def frame_words(cols):
-            j0 = max(start for start in gathered if start <= cols.start)
-            return gathered[j0][:, cols.start - j0 : cols.stop - j0].bitcast(FP8X4)
+        def gather(tiles, window, j0, width):
+            nc.vector.tensor_copy(piece(tiles, j0, width), window.indirect(offsets[:, j0 // 16 : (j0 + width) // 16]))
 
         def gather_scales(j0, width):
-            picks = offsets[:, j0 // 16 : (j0 + width) // 16]
-            nc.vector.tensor_copy(frame_plane[:, j0 : j0 + width], table_plane[:].bitcast(U8).indirect(picks))
+            gather(frame_planes, table_plane[:].bitcast(U8), j0, width)
 
-        grouped = {}
-        packed = {}
+        def gather_words(j0, width):
+            gather(frame_words, table[:].bitcast(U32), j0, width)
 
-        for name in ("co", "si"):
-            for b in range(2):
-                grouped[name, b] = keep.tile(
-                    [P, 2, 2, P, PACK], BF16, name="grouped_%s%d" % (name, b), align_bytes=64
-                )
-                packed[name, b] = (
-                    keep.tile([P, PASS], U32, name="words_%s%d" % (name, b), align_bytes=64),
-                    keep.tile([P, PASS], U8, name="plane_%s%d" % (name, b), align_bytes=64),
-                )
+        def frames(j0, width):
+            return piece(frame_words, j0, width).bitcast(FP8X4), piece(frame_planes, j0, width)
 
-        def cast(engine_copy, name, b, half, pair=None):
-            dst = grouped[name, b][:, :, :, half * 64 : (half + 1) * 64, :].rearrange("p u e m i -> p u m i e")
-            src = halves[name, b, half][:].rearrange("p i (m u e) -> p u m i e", u=2, e=2)
-            if pair is None:
-                engine_copy(dst, src)
-            else:
-                engine_copy(dst[:, pair], src[:, pair])
+        packed = {
+            (name, b): (sbuf([P, PASS], U32, "words_%s%d" % (name, b)), sbuf([P, PASS], U8, "plane_%s%d" % (name, b)))
+            for name in ("co", "si")
+            for b in range(2)
+        }
+        rounded_co0 = sbuf([P, 2, 2, P, PACK], BF16, "rounded_co0")
+        rounded = {
+            (name, b, pair): sbuf([P, 2, P, PACK], BF16, "rounded_%s%d_%d" % (name, b, pair))[:]
+            for name, b in raw
+            for pair in range(2)
+            if (name, b, pair) != ("si", 1, 0)
+        }
+        for pair in range(2):
+            rounded["co", 0, pair] = rounded_co0[:, pair]
+        early = sbuf([P, 3 * PASS], BF16, "early")
+        rounded["si", 1, 0] = early[:, PASS:].rearrange("p (e m i) -> p e m i", e=2, i=PACK)
 
-        def cast_half(engine_copy, name, b, half):
-            engine_copy(
-                grouped[name, b][:, :, :, half * 64 : (half + 1) * 64, :].rearrange("p u e m i -> p m i (u e)"),
-                halves[name, b, half][:].rearrange("p i (m t) -> p m i t", t=PACK),
-            )
+        def frames_of(flat, first, width):
+            return flat[:, first * PACK : (first + width) * PACK].rearrange("p (j t) -> p j t", t=PACK)
 
-        def cast_band(engine_copy, name, b, pair, rows=slice(0, P)):
-            engine_copy(
-                grouped[name, b][:, pair].rearrange("p e m i -> p m i e")[:, rows],
-                whole[name, b][:].rearrange("p i (m u e) -> p u m i e", u=2, e=2)[:, pair, rows],
-            )
-
-        def quantize_weight(name, b, pair):
+        def weight(name, b, c0, width):
             words, plane = packed[name, b]
-            cols = slice(pair * 2 * P, (pair + 1) * 2 * P)
-            nc.vector.quantize_mx(
-                out=words[:, cols].bitcast(FP8X4),
-                scales=plane[:, cols],
-                in_=grouped[name, b][:, pair].rearrange("p e m i -> p (e m i)"),
-            )
+            return words[:, c0 : c0 + width].bitcast(FP8X4), plane[:, c0 : c0 + width]
+
+        def quantize(dst, src):
+            nc.vector.quantize_mx(out=dst[0], scales=dst[1], in_=src)
+
+        def quantize_band(name, b):
+            for pair in range(2):
+                quantize(weight(name, b, pair * HALF, HALF), rounded[name, b, pair].rearrange("p e m i -> p (e m i)"))
+
+        def prepare_band(name, b):
+            for pair in range(2):
+                nc.vector.tensor_copy(
+                    rounded[name, b, pair].rearrange("p e m i -> p m i e"),
+                    raw[name, b][:].rearrange("p i (m u e) -> p u m i e", u=2, e=2)[:, pair],
+                )
+            quantize_band(name, b)
 
         taken = []
 
@@ -160,324 +154,222 @@ def tile_list_meltab_mix_pow_kernel(
             taken.append(shape)
             return sums.tile(shape, F32, name="bank%d" % (len(taken) % SUM_BANKS))
 
-        def transform(bank_cols, name, b, t, j0, width):
-            w_words, w_plane = packed[name, b]
-            cols = slice(j0, j0 + width)
+        def product(dst, stationary, moving, start=True, stop=True):
             nc.tensor.matmul_mx(
-                out=bank_cols,
-                lhsT=w_words[:, t * P : (t + 1) * P].bitcast(FP8X4),
-                lhsT_scale=w_plane[:, t * P : (t + 1) * P],
-                rhs=frame_words(cols),
-                rhs_scale=frame_plane[:, cols],
-                start=True,
-                stop=True,
+                out=dst,
+                lhsT=stationary[0],
+                lhsT_scale=stationary[1],
+                rhs=moving[0],
+                rhs_scale=moving[1],
+                start=start,
+                stop=stop,
             )
-
-        squares = {}
-
-        def square_tile(b, j0, width):
-            squares[b, j0] = keep.tile([P, 2, width // LINE, PACK, LINE], F32, name="squares%d_%d" % (b, j0))
 
         by_frame = {}
 
         def square_by_frame(name, b, jt):
-            w_words, w_plane = packed[name, b]
-            cols = slice(jt * P, (jt + 1) * P)
-            bank = next_bank([P, PASS])
-            nc.tensor.matmul_mx(
-                out=bank[:],
-                lhsT=frame_words(cols),
-                lhsT_scale=frame_plane[:, cols],
-                rhs=w_words[:].bitcast(FP8X4),
-                rhs_scale=w_plane[:],
-                start=True,
-                stop=True,
-            )
-            by_frame[name, b, jt] = keep.tile([P, PASS], F32, name="by_frame_%s%d_%d" % (name, b, jt))
-            nc.scalar.activation(by_frame[name, b, jt][:], bank[:], ACT.Square)
+            bank = next_bank([P, PACK, P])
+            product(bank[:].rearrange("p t m -> p (t m)"), frames(jt * P, P), weight(name, b, 0, PASS))
+            tile = sbuf([P, PACK, P], F32, "by_frame_%s%d_%d" % (name, b, jt))
+            by_frame[name, b, jt] = tile[:]
+            nc.scalar.activation(tile[:], bank[:], ACT.Square)
 
-        def square_two_tiles(name, b, jt, pair):
-            w_words, w_plane = packed[name, b]
-            slots = slice(pair * 2 * P, (pair + 1) * 2 * P)
-            bank = next_bank([P, 2, 2 * P])
-            if pair == 0:
-                both = keep.tile([P, 2, PASS], F32, name="two_tiles_%s%d_%d" % (name, b, jt))
-                two_tiles[name, b, jt] = both
-                for a in range(2):
-                    by_frame[name, b, jt + a] = both[:, a]
-            for a in range(2):
-                cols = slice((jt + a) * P, (jt + a + 1) * P)
-                nc.tensor.matmul_mx(
-                    out=bank[:, a, :],
-                    lhsT=frame_words(cols),
-                    lhsT_scale=frame_plane[:, cols],
-                    rhs=w_words[:, slots].bitcast(FP8X4),
-                    rhs_scale=w_plane[:, slots],
-                    start=True,
-                    stop=True,
-                )
-            nc.scalar.activation(two_tiles[name, b, jt][:, :, slots], bank[:], ACT.Square)
-
-        two_tiles = {}
         turning = {}
 
-        def turn(names, b, jt, opens, closes):
+        def turn(names, b, jt):
+            opens = (b, jt) not in turning
             if opens:
-                turning[b, jt] = results.tile([P, PACK, P], F32, name="acc%d" % (len(turning) % 3))
-            steps = [(name, t) for name in names for t in reversed(range(PACK))]
-            for name, t in steps:
+                turning[b, jt] = turns.tile([P, PACK, P], F32, name="turn%d" % (len(turning) % TURN_BANKS))
+            steps = [(name, t) for name in names for t in range(PACK)]
+            for step in steps:
                 nc.tensor.matmul(
-                    turning[b, jt][:, t, :],
-                    by_frame[name, b, jt][:, t * P : (t + 1) * P],
+                    turning[b, jt][:, step[1], :],
+                    by_frame[step[0], b, jt][:, step[1], :],
                     identity[:],
-                    start=opens and (name, t) == steps[0],
-                    stop=closes and (name, t) == steps[-1],
+                    start=opens and step == steps[0],
+                    stop="si" in names and step == steps[-1],
                     is_transpose=True,
                 )
 
-        power = [keep.tile([P, J, PACK], BF16, name="power%d" % b, align_bytes=64) for b in range(2)]
-
-        def scale_turned(b, jt):
+        def scale_turned(dst, b, jt):
             nc.vector.tensor_tensor(
-                power[b][:, jt * P : (jt + 1) * P, :],
+                dst,
                 turning[b, jt][:].rearrange("p t j -> p j t"),
                 gain[:, b].unsqueeze(1).to_broadcast([P, P, PACK]),
                 ALU.mult,
             )
 
-        def close_turn(b, jt):
-            if (b, jt) in turning:
-                turn(("si",), b, jt, False, True)
-            else:
-                turn(("si", "co"), b, jt, True, True)
+        squares = {}
 
-        def turn_and_scale(b, jt):
-            close_turn(b, jt)
-            scale_turned(b, jt)
-
-        def square_slot(name, b, base, t):
-            bank = next_bank([P, PASS])
-            transform(bank[:], name, b, t, base, PASS)
-            nc.scalar.activation(
-                squares[b, base][:, ("co", "si").index(name), :, t, :],
-                bank[:].rearrange("p (c i) -> p c i", i=LINE),
-                ACT.Square,
-                scale=root[:, b * PACK + t : b * PACK + t + 1],
-            )
-
-        def square_pair(b, j0, t):
-            width = PASS // 2
-            bank = next_bank([P, PASS])
-            transform(bank[:, :width], "co", b, t, j0, width)
-            transform(bank[:, width:], "si", b, t, j0, width)
-            nc.scalar.activation(
-                squares[b, j0][:, :, :, t, :].rearrange("p s c i -> p (s c) i"),
-                bank[:].rearrange("p (c i) -> p c i", i=LINE),
-                ACT.Square,
-                scale=root[:, b * PACK + t : b * PACK + t + 1],
-            )
-
-        def square_duo(name, b, base, j0, t0):
-            width = PASS // 2
-            if (name, t0) == ("si", 2):
-                bank = results.tile([P, 2, width], F32, name="acc2")
-            else:
-                bank = next_bank([P, 2, width])
-            rows = slice((j0 - base) // LINE, (j0 - base + width) // LINE)
-            for t in range(2):
-                transform(bank[:, t, :], name, b, t0 + t, j0, width)
-            for t in range(2):
+        def square_slots(b, j0, width, parts, bank=None):
+            if (b, j0) not in squares:
+                squares[b, j0] = sbuf([P, 2, width // LINE, PACK, LINE], F32, "squares%d_%d" % (b, j0))
+            if bank is None:
+                bank = next_bank([P, len(parts), width])
+            for place, (name, t) in enumerate(parts):
+                product(bank[:, place], weight(name, b, t * P, P), frames(j0, width))
+            for t in sorted(set(slot for name, slot in parts)):
+                places = [place for place, part in enumerate(parts) if part[1] == t]
+                first = ("co", "si").index(parts[places[0]][0])
                 nc.scalar.activation(
-                    squares[b, base][:, ("co", "si").index(name), rows, t0 + t, :],
-                    bank[:, t].rearrange("p (c i) -> p c i", i=LINE),
+                    squares[b, j0][:, first : first + len(places), :, t, :].rearrange("p s c i -> p (s c) i"),
+                    bank[:, places[0] : places[-1] + 1].rearrange("p s (c i) -> p (s c) i", i=LINE),
                     ACT.Square,
-                    scale=root[:, b * PACK + t0 + t : b * PACK + t0 + t + 1],
+                    scale=root[:, b * PACK + t : b * PACK + t + 1],
                 )
 
-        def square_quad(b, j0, t0):
-            bank = next_bank([P, 2, 2, P])
-            for t in range(2):
-                transform(bank[:, t, 0, :], "co", b, t0 + t, j0, P)
-                transform(bank[:, t, 1, :], "si", b, t0 + t, j0, P)
-            for t in range(2):
-                nc.scalar.activation(
-                    squares[b, j0][:, :, :, t0 + t, :].rearrange("p s c i -> p (s c) i"),
-                    bank[:, t].rearrange("p s (c i) -> p (s c) i", i=LINE),
-                    ACT.Square,
-                    scale=root[:, b * PACK + t0 + t : b * PACK + t0 + t + 1],
-                )
+        def square_unit(b, j0):
+            for t in range(PACK):
+                square_slots(b, j0, 256, [("co", t), ("si", t)])
 
-        unsigned = {}
-
-        def add(b, j0, width, whole_width=None):
-            whole_width = whole_width or width
-            first = j0 - j0 % whole_width
-            if (b, first) not in unsigned:
-                unsigned[b, first] = keep.tile(
-                    [P, whole_width, PACK], BF16, name="unsigned%d_%d" % (b, first), align_bytes=64
-                )
-            base = max(start for (half, start) in squares if half == b and start <= j0)
-            rows = slice((j0 - base) // LINE, (j0 - base + width) // LINE)
-            nc.vector.tensor_tensor(
-                unsigned[b, first][:, j0 - first : j0 - first + width].rearrange("p (c i) t -> p c t i", i=LINE),
-                squares[b, base][:, 0, rows],
-                squares[b, base][:, 1, rows],
+        def add(engine, dst, b, j0, first):
+            rows = slice(first // LINE, (first + dst.shape[1]) // LINE)
+            engine.tensor_tensor(
+                dst.rearrange("p (c i) t -> p c t i", i=LINE),
+                squares[b, j0][:, 0, rows],
+                squares[b, j0][:, 1, rows],
                 ALU.add,
             )
 
-        def apply_sign(b, j0, width):
-            nc.vector.tensor_tensor(
-                power[b][:, j0 : j0 + width, :],
-                unsigned[b, j0][:],
-                sign[:, b * PACK : (b + 1) * PACK].unsqueeze(1).to_broadcast([P, width, PACK]),
-                ALU.mult,
-            )
+        def apply_sign(dst, src, b):
+            signs = sign[:, b * PACK : (b + 1) * PACK].unsqueeze(1).to_broadcast(list(dst.shape))
+            nc.vector.tensor_tensor(dst, src, signs, ALU.mult)
 
-        power_words = [keep.tile([P, J], U32, name="power_words%d" % b, align_bytes=64) for b in range(2)]
-        power_plane = [keep.tile([P, J], U8, name="power_plane%d" % b, align_bytes=64) for b in range(2)]
+        def rounded_power(width, name, tag=None):
+            return sbuf([P, width, PACK], BF16, name, tag)[:]
 
-        def quantize_power(b, j0, width):
-            nc.vector.quantize_mx(
-                out=power_words[b][:, j0 : j0 + width].bitcast(FP8X4),
-                scales=power_plane[b][:, j0 : j0 + width],
-                in_=power[b][:, j0 : j0 + width, :].rearrange("p j t -> p (j t)"),
-            )
+        power_words = [sbuf([P, J], U32, "power_words%d" % b) for b in range(2)]
+        power_plane = [sbuf([P, J], U8, "power_plane%d" % b) for b in range(2)]
 
-        fb_bytes = fb_plane[:].bitcast(U8)
+        def power_codes(b, j0, width):
+            return power_words[b][:, j0 : j0 + width].bitcast(FP8X4), power_plane[b][:, j0 : j0 + width]
 
-        def filter_pass(dst, b, nt, cols, start, stop):
+        def quantize_power(src, b, j0):
+            quantize(power_codes(b, j0, src.shape[1]), src.rearrange("p j t -> p (j t)"))
+
+        def filters(b, nt):
             if b == 0:
                 codes = fb8[:, nt * P : (nt + 1) * P].bitcast(FP8X4)
             else:
                 codes = fb4[:].bitcast(U8)[:, nt * 2 * P : (nt + 1) * 2 * P].bitcast(FP4X4)
-            nc.tensor.matmul_mx(
-                out=dst,
-                lhsT=codes,
-                lhsT_scale=fb_bytes[:, b * N + nt * P : b * N + (nt + 1) * P],
-                rhs=power_words[b][:, cols].bitcast(FP8X4),
-                rhs_scale=power_plane[b][:, cols],
-                start=start,
-                stop=stop,
-            )
+            return codes, fb_plane[:].bitcast(U8)[:, b * N + nt * P : b * N + (nt + 1) * P]
 
-        filtered = {}
-
-        def filter_block(j0, width):
+        def filter_bank(j0, width, engine_copy):
             acc = next_bank([P, N // P, width])
-            steps = [(b, g0, nt) for b in range(2) for g0 in range(0, width, min(GROUP, width)) for nt in range(N // P)]
-            for step in steps:
-                b, g0, nt = step
-                cols = slice(j0 + g0, j0 + g0 + min(GROUP, width))
-                filter_pass(acc[:, nt, g0 : g0 + min(GROUP, width)], b, nt, cols, step == steps[0], step == steps[-1])
-            filtered[j0] = (acc, width)
-
-        def store_block(j0, engine_copy):
-            acc, width = filtered[j0]
-            staged = keep.tile([P, N // P, width], F32, name="staged%d" % j0)
+            steps = [(b, nt) for b in range(2) for nt in range(N // P)]
+            for b, nt in steps:
+                product(acc[:, nt], filters(b, nt), power_codes(b, j0, width), (b, nt) == steps[0], (b, nt) == steps[-1])
+            staged = sbuf([P, N // P, width], F32, "staged%d" % j0)
             engine_copy(staged[:], acc[:])
             nc.sync.dma_start(out=out.rearrange("(a p) j -> p a j", p=P)[:, :, j0 : j0 + width], in_=staged[:])
 
-        def filter_bank(j0, width, engine_copy=nc.scalar.copy):
-            filter_block(j0, width)
-            store_block(j0, engine_copy)
-
         def filter_last(j0):
-            cols = slice(j0, j0 + P)
-            accs = [results.tile([P, P], F32, name="acc%d" % nt) for nt in range(N // P)]
+            accs = [turns.tile([P, P], F32, name="turn%d" % nt) for nt in range(N // P)]
             for b in range(2):
                 for nt in range(N // P):
-                    filter_pass(accs[nt][:], b, nt, cols, b == 0, b == 1)
-            for nt, (engine_copy, queue) in enumerate(((nc.scalar.copy, nc.sync), (nc.vector.tensor_copy, nc.sync))):
-                staged = keep.tile([P, P], F32, name="last%d" % nt)
+                    product(accs[nt][:], filters(b, nt), power_codes(b, j0, P), b == 0, b == 1)
+            for nt, engine_copy in enumerate((nc.scalar.copy, nc.vector.tensor_copy)):
+                staged = sbuf([P, P], F32, "last%d" % nt)
                 engine_copy(staged[:], accs[nt][:])
-                queue.dma_start(out=out[nt * P : (nt + 1) * P, cols], in_=staged[:])
+                nc.sync.dma_start(out=out[nt * P : (nt + 1) * P, j0 : j0 + P], in_=staged[:])
 
+        frame_planes[0] = sbuf([P, J], U8, "frame_plane0")
+        gather_scales(0, J)
+        for h in range(2):
+            nc.scalar.copy(
+                rounded_co0[:, :, :, h * 64 : (h + 1) * 64, :].rearrange("p u e m i -> p m i (u e)"),
+                raw_half[h][:].rearrange("p i (m t) -> p m i t", t=PACK),
+            )
+        quantize_band("co", 0)
+        for j0, width in ((0, P), (P, P), (256, 256), (512, 256)):
+            frame_words[j0] = sbuf([P, width], U32, "frame_words%d" % j0)
+            gather_words(j0, width)
+        prepare_band("si", 0)
+        frame_words[768] = sbuf([P, 256], U32, "frame_words768", "raw_si0")
+        gather_words(768, 256)
+        prepare_band("co", 1)
 
-        gather_scales(0, 1024)
-        cast_half(nc.scalar.copy, "co", 0, 0)
-        cast_half(nc.scalar.copy, "co", 0, 1)
-        quantize_weight("co", 0, 0)
-        quantize_weight("co", 0, 1)
-        gather_words(0, 128)
-        gather_words(128, 128)
-        gather_words(256, 256)
-        gather_words(512, 256)
-        for pair in range(2):
-            cast_band(nc.vector.tensor_copy, "si", 0, pair)
-        for pair in range(2):
-            quantize_weight("si", 0, pair)
-        gather_words(768, 256, "si0_then_frames")
-        for pair in range(2):
-            cast_band(nc.vector.tensor_copy, "co", 1, pair)
-        for pair in range(2):
-            quantize_weight("co", 1, pair)
-
-        square_tile(0, 512, 256)
-        square_tile(0, 768, 256)
-        square_tile(1, 512, 256)
-        square_tile(1, 896, 128)
         for jt in range(4):
             square_by_frame("co", 0, jt)
-        for name in ("co", "si"):
-            for t0 in (0, 2):
-                square_duo(name, 0, 512, 512, t0)
-        for jt in range(3):
-            turn(("co",), 0, jt, True, False)
-        for pair in range(2):
-            cast_band(nc.vector.tensor_copy, "si", 1, pair)
-        for pair in range(2):
-            quantize_weight("si", 1, pair)
-        for pair in range(2):
-            square_two_tiles("si", 0, 0, pair)
-        for jt in (2, 3):
+        for t0 in (0, 2):
+            square_slots(0, 512, 256, [("co", t0), ("co", t0 + 1)])
+        square_slots(0, 512, 256, [("si", 0), ("si", 1)])
+        square_slots(0, 512, 256, [("si", 2), ("si", 3)], turns.tile([P, 2, 256], F32, name="turn2"))
+        for jt in range(TURN_BANKS):
+            turn(("co",), 0, jt)
+        add(nc.vector, frames_of(early, P - OWN, OWN), 0, 512, 0)
+        prepare_band("si", 1)
+        for jt in range(4):
             square_by_frame("si", 0, jt)
-        for t in range(PACK):
-            square_pair(0, 768, t)
-            if t >= 1:
-                for jt in ((0, 1), (2,), (3,))[t - 1]:
-                    turn_and_scale(0, jt)
-        square_by_frame("co", 1, 0)
-        square_by_frame("si", 1, 0)
-        square_pair(1, 512, 0)
-        square_by_frame("co", 1, 1)
-        square_by_frame("si", 1, 1)
-        square_pair(1, 512, 1)
-        turn_and_scale(1, 0)
-        square_by_frame("co", 1, 2)
-        square_by_frame("si", 1, 2)
-        square_pair(1, 512, 2)
-        turn_and_scale(1, 1)
-        square_pair(1, 512, 3)
-        square_by_frame("co", 1, 3)
-        square_by_frame("si", 1, 3)
-        close_turn(1, 2)
-        square_by_frame("co", 1, 6)
-        square_by_frame("si", 1, 6)
-        square_quad(1, 896, 0)
-        square_quad(1, 896, 2)
-        close_turn(1, 3)
-        close_turn(1, 6)
+        square_unit(0, 768)
+        for jt in range(TURN_BANKS):
+            turn(("si",), 0, jt)
 
-        add(0, 512, 256, 512)
-        add(0, 768, 256, 512)
-        apply_sign(0, 512, 512)
-        quantize_power(0, 0, 1024)
-        quantize_power(1, 0, 256)
-        add(1, 512, 256)
-        apply_sign(1, 512, 256)
-        scale_turned(1, 2)
-        quantize_power(1, 512, 256)
-        quantize_power(1, 256, 128)
-        scale_turned(1, 3)
-        add(1, 896, 128)
-        quantize_power(1, 384, 128)
-        scale_turned(1, 6)
-        apply_sign(1, 896, 128)
-        quantize_power(1, 768, 128)
-        quantize_power(1, 896, 128)
-        filter_bank(0, 256)
-        filter_bank(512, 256)
-        filter_bank(256, 128)
-        filter_bank(384, 128)
-        filter_bank(768, 128, nc.vector.tensor_copy)
+        add(nc.gpsimd, frames_of(early, P, 256 - OWN), 0, 512, OWN)
+        turned = rounded_power(4 * P, "turned0", "raw_si1")
+        for jt in range(TURN_BANKS):
+            scale_turned(turned[:, jt * P : (jt + 1) * P], 0, jt)
+        turn(("co", "si"), 0, 3)
+        unit = frames_of(early, P - OWN, 256)
+        apply_sign(unit, unit, 0)
+        second = rounded_power(256, "unit768")
+        add(nc.vector, second, 0, 768, 0)
+        quantize_power(unit, 0, 512)
+        scale_turned(turned[:, 3 * P :], 0, 3)
+        apply_sign(second, second, 0)
+
+        def square_tile(jt):
+            for name in ("co", "si"):
+                square_by_frame(name, 1, jt)
+
+        def square_pair(t):
+            square_slots(1, 512, 256, [("co", t), ("si", t)])
+
+        power1 = rounded_power(J, "power1")
+
+        def scale_tile(jt):
+            scale_turned(power1[:, jt * P : (jt + 1) * P], 1, jt)
+
+        def quantize_frames(j0, width):
+            quantize_power(power1[:, j0 : j0 + width], 1, j0)
+
+        def add_frames(j0, width):
+            add(nc.vector, power1[:, j0 : j0 + width], 1, j0, 0)
+
+        def sign_frames(j0, width):
+            apply_sign(power1[:, j0 : j0 + width], power1[:, j0 : j0 + width], 1)
+
+        for jt in range(3):
+            square_tile(jt)
+            square_pair(jt)
+            if jt >= 1:
+                turn(("co", "si"), 1, jt - 1)
+                scale_tile(jt - 1)
+        square_pair(3)
+        square_tile(3)
+        turn(("co", "si"), 1, 2)
+        square_tile(6)
+        for t0 in (0, 2):
+            square_slots(1, 896, P, [(name, t) for t in (t0, t0 + 1) for name in ("co", "si")])
+        turn(("co", "si"), 1, 3)
+        turn(("co", "si"), 1, 6)
+
+        quantize_power(turned, 0, 0)
+        quantize_power(second, 0, 768)
+        quantize_frames(0, 256)
+        add_frames(512, 256)
+        sign_frames(512, 256)
+        scale_tile(2)
+        quantize_frames(512, 256)
+        quantize_frames(256, P)
+        scale_tile(3)
+        add_frames(896, P)
+        quantize_frames(384, P)
+        scale_tile(6)
+        sign_frames(896, P)
+        quantize_frames(768, P)
+        quantize_frames(896, P)
+        for j0, width in ((0, 256), (512, 256), (256, P), (384, P)):
+            filter_bank(j0, width, nc.scalar.copy)
+        filter_bank(768, P, nc.vector.tensor_copy)
         filter_last(896)

@@ -24,7 +24,6 @@ HALF = PASS // 2
 LINE = 4
 SUM_BANKS = 5
 TURN_BANKS = 3
-OWN = 128
 
 
 def load_scale_rows(queue, plane, rows):
@@ -52,7 +51,9 @@ def tile_list_meltab_mix_pow_kernel(
         fb4 = sbuf([P, N // 2], I32, "fb4")
         gain = sbuf([P, 2, PACK], F32, "gain")
 
+        gain_rows = sbuf([P, PASS], F32, "gain_rows")
         nc.gpsimd.memset(table_plane[:], 0)
+        nc.gpsimd.memset(gain_rows[:], 0.0)
         nc.gpsimd.memset(fb_plane[:], 0)
 
         def load_columns(matrix, f0, width, name):
@@ -61,15 +62,15 @@ def tile_list_meltab_mix_pow_kernel(
             return tile
 
         nc.sync.dma_start(offsets[:], offs)
-        nc.sync.dma_start(out=gain[:], in_=gn.rearrange("(b p t) -> p b t", b=2, t=PACK))
         raw_half = [load_columns(co, 0, HALF, "raw_half0")]
         load_scale_rows(nc.sync, table_plane, tab_scales[0])
+        nc.sync.dma_start(out=gain_rows[0:2, :], in_=gn.rearrange("(b f) -> b f", b=2))
         raw_half.append(load_columns(co, HALF, HALF, "raw_half1"))
         nc.sync.dma_start(out=table[:], in_=tab_words[0].rearrange("p t i -> p (t i)").bitcast(I32))
         raw = {
-            ("si", 0): load_columns(si, 0, PASS, "raw_si0"),
-            ("co", 1): load_columns(co, PASS, PASS, "raw_co1"),
-            ("si", 1): load_columns(si, PASS, PASS, "raw_si1"),
+            ("si", 0): load_columns(si, 0, PASS, "raw_si0")[:],
+            ("co", 1): load_columns(co, PASS, PASS, "raw_co1")[:],
+            ("si", 1): load_columns(si, PASS, PASS, "raw_si1")[:],
         }
         nc.sync.dma_start(out=fb8[:], in_=fb8_words[0].rearrange("p n i -> p (n i)").bitcast(I32))
         nc.sync.dma_start(out=fb4[:], in_=fb4_words[0].bitcast(I32))
@@ -78,17 +79,11 @@ def tile_list_meltab_mix_pow_kernel(
 
         identity = sbuf([P, P], F32, "identity")
         make_identity(nc, identity[:])
-        size = sbuf([P, 2 * PACK], F32, "size")
-        twice = sbuf([P, 2 * PACK], F32, "twice")
         half_power = sbuf([P, 2 * PACK], F32, "half_power")
-        root = sbuf([P, 2 * PACK], F32, "root")
-        sign = sbuf([P, 2 * PACK], BF16, "sign")
         nc.gpsimd.memset(half_power[:], 0.5)
-        flat_gain = gain[:].rearrange("p b t -> p (b t)")
-        nc.gpsimd.tensor_scalar(twice[:], flat_gain, 0.0, 2.0, ALU.is_ge, ALU.mult)
-        nc.gpsimd.tensor_scalar(sign[:], twice[:], 1.0, -1.0, ALU.mult, ALU.add)
-        nc.gpsimd.tensor_tensor(size[:], flat_gain, sign[:], ALU.mult)
-        nc.gpsimd.tensor_tensor(root[:], size[:], half_power[:], ALU.pow)
+        spread = turns.tile([P, PACK, P], F32, name="turn0")
+        for t in range(PACK):
+            nc.tensor.transpose(spread[:, t, :], gain_rows[:].rearrange("p (m t) -> p t m", t=PACK)[:, t], identity[:])
 
         frame_planes = {}
         frame_words = {}
@@ -114,20 +109,9 @@ def tile_list_meltab_mix_pow_kernel(
             for name in ("co", "si")
             for b in range(2)
         }
-        rounded_co0 = sbuf([P, 2, 2, P, PACK], BF16, "rounded_co0")
-        rounded = {
-            (name, b, pair): sbuf([P, 2, P, PACK], BF16, "rounded_%s%d_%d" % (name, b, pair))[:]
-            for name, b in raw
-            for pair in range(2)
-            if (name, b, pair) != ("si", 1, 0)
-        }
-        for pair in range(2):
-            rounded["co", 0, pair] = rounded_co0[:, pair]
-        early = sbuf([P, 3 * PASS], BF16, "early")
-        rounded["si", 1, 0] = early[:, PASS:].rearrange("p (e m i) -> p e m i", e=2, i=PACK)
-
-        def frames_of(flat, first, width):
-            return flat[:, first * PACK : (first + width) * PACK].rearrange("p (j t) -> p j t", t=PACK)
+        rounded = {key: sbuf([P, 2, 2, P, PACK], BF16, "rounded_%s%d" % key) for key in packed if key != ("si", 1)}
+        shared = sbuf([P, J * PACK], BF16, "shared")
+        rounded["si", 1] = shared[:, PASS : 5 * PASS].rearrange("p (u e m i) -> p u e m i", u=2, e=2, i=PACK)
 
         def weight(name, b, c0, width):
             words, plane = packed[name, b]
@@ -136,17 +120,21 @@ def tile_list_meltab_mix_pow_kernel(
         def quantize(dst, src):
             nc.vector.quantize_mx(out=dst[0], scales=dst[1], in_=src)
 
-        def quantize_band(name, b):
+        def quantize_by_pairs(name, b):
             for pair in range(2):
-                quantize(weight(name, b, pair * HALF, HALF), rounded[name, b, pair].rearrange("p e m i -> p (e m i)"))
+                quantize(weight(name, b, pair * HALF, HALF), rounded[name, b][:, pair].rearrange("p e m i -> p (e m i)"))
 
-        def prepare_band(name, b):
+        def cast_views(name, b):
+            return (
+                rounded[name, b][:, :].rearrange("p u e m i -> p u m i e"),
+                raw[name, b].rearrange("p i (m u e) -> p u m i e", u=2, e=2),
+            )
+
+        def prepare_by_pairs(name, b):
+            dst, src = cast_views(name, b)
             for pair in range(2):
-                nc.vector.tensor_copy(
-                    rounded[name, b, pair].rearrange("p e m i -> p m i e"),
-                    raw[name, b][:].rearrange("p i (m u e) -> p u m i e", u=2, e=2)[:, pair],
-                )
-            quantize_band(name, b)
+                nc.vector.tensor_copy(dst[:, pair], src[:, pair])
+            quantize_by_pairs(name, b)
 
         taken = []
 
@@ -277,99 +265,105 @@ def tile_list_meltab_mix_pow_kernel(
         gather_scales(0, J)
         for h in range(2):
             nc.scalar.copy(
-                rounded_co0[:, :, :, h * 64 : (h + 1) * 64, :].rearrange("p u e m i -> p m i (u e)"),
+                rounded["co", 0][:, :, :, h * 64 : (h + 1) * 64, :].rearrange("p u e m i -> p m i (u e)"),
                 raw_half[h][:].rearrange("p i (m t) -> p m i t", t=PACK),
             )
-        quantize_band("co", 0)
-        for j0, width in ((0, P), (P, P), (256, 256), (512, 256)):
+        quantize_by_pairs("co", 0)
+        by_band = spread[:, :, 0:2].rearrange("p t b -> p b t")
+        size = sbuf([P, 2 * PACK], F32, "size")
+        sign = sbuf([P, 2 * PACK], BF16, "sign")
+        root = sbuf([P, 2 * PACK], F32, "root", "rounded_co0")
+        nc.scalar.activation(size[:].rearrange("p (b t) -> p b t", b=2), by_band, ACT.Abs)
+        nc.scalar.activation(sign[:].rearrange("p (b t) -> p b t", b=2), by_band, ACT.Sign)
+        nc.scalar.copy(gain[:], by_band)
+        nc.gpsimd.tensor_tensor(root[:], size[:], half_power[:], ALU.pow)
+        for j0, width in ((256, P), (384, P), (512, 256), (0, 256)):
             frame_words[j0] = sbuf([P, width], U32, "frame_words%d" % j0)
             gather_words(j0, width)
-        prepare_band("si", 0)
+        prepare_by_pairs("si", 0)
         frame_words[768] = sbuf([P, 256], U32, "frame_words768", "raw_si0")
         gather_words(768, 256)
-        prepare_band("co", 1)
+        prepare_by_pairs("co", 1)
 
-        for jt in range(4):
+        for jt in range(2, 6):
             square_by_frame("co", 0, jt)
         for t0 in (0, 2):
-            square_slots(0, 512, 256, [("co", t0), ("co", t0 + 1)])
-        square_slots(0, 512, 256, [("si", 0), ("si", 1)])
-        square_slots(0, 512, 256, [("si", 2), ("si", 3)], turns.tile([P, 2, 256], F32, name="turn2"))
-        for jt in range(TURN_BANKS):
+            square_slots(0, 0, 256, [("co", t0), ("co", t0 + 1)])
+        square_slots(0, 0, 256, [("si", 0), ("si", 1)])
+        square_slots(0, 0, 256, [("si", 2), ("si", 3)], turns.tile([P, 2, 256], F32, name="turn2"))
+        for jt in range(2, 5):
             turn(("co",), 0, jt)
-        add(nc.vector, frames_of(early, P - OWN, OWN), 0, 512, 0)
-        prepare_band("si", 1)
-        for jt in range(4):
+        power = [
+            shared[:].rearrange("p (j t) -> p j t", t=PACK),
+            rounded_power(J, "power1"),
+        ]
+
+        def scale_tile(b, jt):
+            scale_turned(power[b][:, jt * P : (jt + 1) * P], b, jt)
+
+        def quantize_frames(b, j0, width):
+            quantize_power(power[b][:, j0 : j0 + width], b, j0)
+
+        def add_frames(engine, b, j0, first, width):
+            add(engine, power[b][:, j0 + first : j0 + first + width], b, j0, first)
+
+        def sign_frames(b, j0, width):
+            apply_sign(power[b][:, j0 : j0 + width], power[b][:, j0 : j0 + width], b)
+
+        add_frames(nc.vector, 0, 0, 0, P)
+        prepare_by_pairs("si", 1)
+        for jt in range(2, 6):
             square_by_frame("si", 0, jt)
         square_unit(0, 768)
-        for jt in range(TURN_BANKS):
+        for jt in range(2, 5):
             turn(("si",), 0, jt)
-
-        add(nc.gpsimd, frames_of(early, P, 256 - OWN), 0, 512, OWN)
-        turned = rounded_power(4 * P, "turned0", "raw_si1")
-        for jt in range(TURN_BANKS):
-            scale_turned(turned[:, jt * P : (jt + 1) * P], 0, jt)
-        turn(("co", "si"), 0, 3)
-        unit = frames_of(early, P - OWN, 256)
-        apply_sign(unit, unit, 0)
-        second = rounded_power(256, "unit768")
-        add(nc.vector, second, 0, 768, 0)
-        quantize_power(unit, 0, 512)
-        scale_turned(turned[:, 3 * P :], 0, 3)
-        apply_sign(second, second, 0)
+        add_frames(nc.gpsimd, 0, 0, P, P)
+        for jt in range(2, 5):
+            scale_tile(0, jt)
+        turn(("co", "si"), 0, 5)
+        sign_frames(0, 0, 256)
+        add_frames(nc.vector, 0, 768, 0, 256)
+        quantize_frames(0, 0, 512)
+        scale_tile(0, 5)
+        sign_frames(0, 768, 256)
 
         def square_tile(jt):
             for name in ("co", "si"):
                 square_by_frame(name, 1, jt)
 
         def square_pair(t):
-            square_slots(1, 512, 256, [("co", t), ("si", t)])
+            square_slots(1, 0, 256, [("co", t), ("si", t)])
 
-        power1 = rounded_power(J, "power1")
-
-        def scale_tile(jt):
-            scale_turned(power1[:, jt * P : (jt + 1) * P], 1, jt)
-
-        def quantize_frames(j0, width):
-            quantize_power(power1[:, j0 : j0 + width], 1, j0)
-
-        def add_frames(j0, width):
-            add(nc.vector, power1[:, j0 : j0 + width], 1, j0, 0)
-
-        def sign_frames(j0, width):
-            apply_sign(power1[:, j0 : j0 + width], power1[:, j0 : j0 + width], 1)
-
-        for jt in range(3):
-            square_tile(jt)
-            square_pair(jt)
-            if jt >= 1:
-                turn(("co", "si"), 1, jt - 1)
-                scale_tile(jt - 1)
+        for t in range(3):
+            square_tile(2 + t)
+            square_pair(t)
+            if t >= 1:
+                turn(("co", "si"), 1, 1 + t)
+                scale_tile(1, 1 + t)
         square_pair(3)
-        square_tile(3)
-        turn(("co", "si"), 1, 2)
+        square_tile(5)
+        turn(("co", "si"), 1, 4)
         square_tile(6)
         for t0 in (0, 2):
             square_slots(1, 896, P, [(name, t) for t in (t0, t0 + 1) for name in ("co", "si")])
-        turn(("co", "si"), 1, 3)
+        turn(("co", "si"), 1, 5)
         turn(("co", "si"), 1, 6)
 
-        quantize_power(turned, 0, 0)
-        quantize_power(second, 0, 768)
-        quantize_frames(0, 256)
-        add_frames(512, 256)
-        sign_frames(512, 256)
-        scale_tile(2)
-        quantize_frames(512, 256)
-        quantize_frames(256, P)
-        scale_tile(3)
-        add_frames(896, P)
-        quantize_frames(384, P)
-        scale_tile(6)
-        sign_frames(896, P)
-        quantize_frames(768, P)
-        quantize_frames(896, P)
-        for j0, width in ((0, 256), (512, 256), (256, P), (384, P)):
+        quantize_frames(0, 512, 512)
+        quantize_frames(1, 256, 256)
+        add_frames(nc.vector, 1, 0, 0, 256)
+        sign_frames(1, 0, 256)
+        scale_tile(1, 4)
+        quantize_frames(1, 0, 256)
+        quantize_frames(1, 512, P)
+        scale_tile(1, 5)
+        add_frames(nc.vector, 1, 896, 0, P)
+        quantize_frames(1, 640, P)
+        scale_tile(1, 6)
+        sign_frames(1, 896, P)
+        quantize_frames(1, 768, P)
+        quantize_frames(1, 896, P)
+        for j0, width in ((256, 256), (0, 256), (512, P), (640, P)):
             filter_bank(j0, width, nc.scalar.copy)
         filter_bank(768, P, nc.vector.tensor_copy)
         filter_last(896)

@@ -24,6 +24,7 @@ HALF = PASS // 2
 LINE = 4
 SUM_BANKS = 5
 TURN_BANKS = 3
+OWN = 176
 
 
 def load_scale_rows(queue, plane, rows):
@@ -322,10 +323,13 @@ def tile_list_meltab_mix_pow_kernel(
             scale_tile(0, jt)
         turn(("co", "si"), 0, 5)
         sign_frames(0, 0, 256)
-        add_frames(nc.vector, 0, 768, 0, 256)
-        quantize_frames(0, 0, 512)
-        scale_tile(0, 5)
-        sign_frames(0, 768, 256)
+        quantize_frames(0, 256, 384)
+        quantize_frames(0, 0, 256)
+        add_frames(nc.vector, 0, 768, 0, OWN)
+        handed = power[0][:, : 256 - OWN]
+        add(nc.gpsimd, handed, 0, 768, OWN)
+        fourth = power[0][:, P : 2 * P]
+        scale_turned(fourth, 0, 5)
 
         def square_tile(jt):
             for name in ("co", "si"):
@@ -340,6 +344,10 @@ def tile_list_meltab_mix_pow_kernel(
             if t >= 1:
                 turn(("co", "si"), 1, 1 + t)
                 scale_tile(1, 1 + t)
+            if t == 1:
+                sign_frames(0, 768, OWN)
+                apply_sign(power[0][:, 768 + OWN :], handed, 0)
+                quantize_power(fourth, 0, 640)
         square_pair(3)
         square_tile(5)
         turn(("co", "si"), 1, 4)
@@ -349,7 +357,7 @@ def tile_list_meltab_mix_pow_kernel(
         turn(("co", "si"), 1, 5)
         turn(("co", "si"), 1, 6)
 
-        quantize_frames(0, 512, 512)
+        quantize_frames(0, 768, 256)
         quantize_frames(1, 256, 256)
         add_frames(nc.vector, 1, 0, 0, 256)
         sign_frames(1, 0, 256)

@@ -335,43 +335,50 @@ def tile_list_meltab_mix_pow_kernel(
             for name in ("co", "si"):
                 square_by_frame(name, 1, jt)
 
+        def square_single(j0):
+            for t0 in (0, 2):
+                square_slots(1, j0, P, [(name, t) for t in (t0, t0 + 1) for name in ("co", "si")])
+
         def square_pair(t):
             square_slots(1, 0, 256, [("co", t), ("si", t)])
 
         for t in range(3):
-            square_tile(2 + t)
-            square_pair(t)
+            if t < 2:
+                square_tile(4 + t)
+                square_pair(t)
+            else:
+                square_single(256)
+                square_pair(t)
             if t >= 1:
-                turn(("co", "si"), 1, 1 + t)
-                scale_tile(1, 1 + t)
+                turn(("co", "si"), 1, 3 + t)
+                scale_tile(1, 3 + t)
             if t == 1:
                 sign_frames(0, 768, OWN)
                 apply_sign(power[0][:, 768 + OWN :], handed, 0)
                 quantize_power(fourth, 0, 640)
         square_pair(3)
-        square_tile(5)
-        turn(("co", "si"), 1, 4)
+        square_tile(3)
         square_tile(6)
-        for t0 in (0, 2):
-            square_slots(1, 896, P, [(name, t) for t in (t0, t0 + 1) for name in ("co", "si")])
-        turn(("co", "si"), 1, 5)
+        square_single(896)
+        turn(("co", "si"), 1, 3)
         turn(("co", "si"), 1, 6)
 
         quantize_frames(0, 768, 256)
-        quantize_frames(1, 256, 256)
+        add_frames(nc.vector, 1, 256, 0, P)
+        quantize_frames(1, 512, 256)
         add_frames(nc.vector, 1, 0, 0, 256)
+        sign_frames(1, 256, P)
         sign_frames(1, 0, 256)
-        scale_tile(1, 4)
+        quantize_frames(1, 256, P)
         quantize_frames(1, 0, 256)
-        quantize_frames(1, 512, P)
-        scale_tile(1, 5)
-        add_frames(nc.vector, 1, 896, 0, P)
-        quantize_frames(1, 640, P)
+        scale_tile(1, 3)
         scale_tile(1, 6)
-        sign_frames(1, 896, P)
+        quantize_frames(1, 384, P)
+        add_frames(nc.vector, 1, 896, 0, P)
         quantize_frames(1, 768, P)
+        sign_frames(1, 896, P)
         quantize_frames(1, 896, P)
-        for j0, width in ((256, 256), (0, 256), (512, P), (640, P)):
+        for j0, width in ((512, 256), (256, P), (0, 256), (384, P)):
             filter_bank(j0, width, nc.scalar.copy)
         filter_bank(768, P, nc.vector.tensor_copy)
         filter_last(896)

@@ -24,7 +24,8 @@ HALF = PASS // 2
 LINE = 4
 SUM_BANKS = 5
 TURN_BANKS = 3
-OWN = 176
+OWN_EARLY = 96
+OWN = 152
 
 
 def load_scale_rows(queue, plane, rows):
@@ -311,14 +312,14 @@ def tile_list_meltab_mix_pow_kernel(
         def sign_frames(b, j0, width):
             apply_sign(power[b][:, j0 : j0 + width], power[b][:, j0 : j0 + width], b)
 
-        add_frames(nc.vector, 0, 0, 0, P)
+        add_frames(nc.vector, 0, 0, 0, OWN_EARLY)
         prepare_by_pairs("si", 1)
         for jt in range(2, 6):
             square_by_frame("si", 0, jt)
         square_unit(0, 768)
         for jt in range(2, 5):
             turn(("si",), 0, jt)
-        add_frames(nc.gpsimd, 0, 0, P, P)
+        add_frames(nc.gpsimd, 0, 0, OWN_EARLY, 256 - OWN_EARLY)
         for jt in range(2, 5):
             scale_tile(0, jt)
         turn(("co", "si"), 0, 5)

from contextlib import ExitStack

import concourse.mybir as mybir
from concourse.masks import make_identity

K, F, N, T, J = 512, 1024, 256, 2048, 1024
FLOPS = 2 * (2 * K * F * J + F * N * J)

F32 = mybir.dt.float32
BF16 = mybir.dt.bfloat16
I32 = mybir.dt.int32
U32 = mybir.dt.uint32
U16 = mybir.dt.uint16
U8 = mybir.dt.uint8
FP8X4 = mybir.dt.float8_e4m3fn_x4
FP4X4 = mybir.dt.float4_e2m1fn_x4
ACT = mybir.ActivationFunctionType
ALU = mybir.AluOpType

P = 128
PACK = 4
PASS = P * PACK
HALF = PASS // 2
LINE = 4
SUM_BANKS = 5
TURN_BANKS = 3
OWN_EARLY = 96
OWN = 152


def load_scale_rows(queue, plane, rows):
    for quad in range(4):
        queue.dma_start(out=plane[32 * quad : 32 * quad + 4, :], in_=rows[4 * quad : 4 * quad + 4, :].bitcast(I32))


def tile_list_meltab_mix_pow_kernel(
    tc, tab_words, tab_scales, co, si, gn, fb8_words, fb8_scales, fb4_words, fb4_scales, offs, out
):
    nc = tc.nc
    with ExitStack() as ctx:
        keep = ctx.enter_context(tc.tile_pool(name="keep", bufs=1))
        sums = ctx.enter_context(tc.psum_pool(name="sums", bufs=1))
        turns = ctx.enter_context(tc.psum_pool(name="turns", bufs=1))

        def sbuf(shape, dtype, name, tag=None):
            return keep.tile(shape, dtype, name=name, tag=tag or name, align_bytes=64)

        offsets = keep.tile([P, J // 16], U16, name="offsets")
        table = sbuf([P, T], I32, "table")
        table_plane = sbuf([P, T // 4], I32, "table_plane")
        fb_plane = sbuf([P, 2 * N // 4], I32, "fb_plane")
        fb8 = sbuf([P, N], I32, "fb8")
        fb4 = sbuf([P, N // 2], I32, "fb4")
        gain = sbuf([P, 2, PACK], F32, "gain")

        gain_rows = sbuf([P, PASS], F32, "gain_rows")
        nc.gpsimd.memset(table_plane[:], 0)
        nc.gpsimd.memset(gain_rows[:], 0.0)
        nc.gpsimd.memset(fb_plane[:], 0)

        def load_columns(matrix, f0, width, name):
            tile = sbuf([P, PACK, width], F32, name)
            nc.sync.dma_start(out=tile[:], in_=matrix.rearrange("(p i) f -> p i f", i=PACK)[:, :, f0 : f0 + width])
            return tile

        nc.sync.dma_start(offsets[:], offs)
        raw_half = [load_columns(co, 0, HALF, "raw_half0")]
        load_scale_rows(nc.sync, table_plane, tab_scales[0])
        nc.sync.dma_start(out=gain_rows[0:2, :], in_=gn.rearrange("(b f) -> b f", b=2))
        raw_half.append(load_columns(co, HALF, HALF, "raw_half1"))
        nc.sync.dma_start(out=table[:], in_=tab_words[0].rearrange("p t i -> p (t i)").bitcast(I32))
        raw = {
            ("si", 0): load_columns(si, 0, PASS, "raw_si0")[:],
            ("co", 1): load_columns(co, PASS, PASS, "raw_co1")[:],
            ("si", 1): load_columns(si, PASS, PASS, "raw_si1")[:],
        }
        nc.sync.dma_start(out=fb8[:], in_=fb8_words[0].rearrange("p n i -> p (n i)").bitcast(I32))
        nc.sync.dma_start(out=fb4[:], in_=fb4_words[0].bitcast(I32))
        load_scale_rows(nc.sync, fb_plane[:, : N // 4], fb8_scales[0])
        load_scale_rows(nc.sync, fb_plane[:, N // 4 :], fb4_scales[0])

        identity = sbuf([P, P], F32, "identity")
        make_identity(nc, identity[:])
        half_power = sbuf([P, 2 * PACK], F32, "half_power")
        nc.gpsimd.memset(half_power[:], 0.5)
        spread = turns.tile([P, PACK, P], F32, name="turn0")
        for t in range(PACK):
            nc.tensor.transpose(spread[:, t, :], gain_rows[:].rearrange("p (m t) -> p t m", t=PACK)[:, t], identity[:])

        frame_planes = {}
        frame_words = {}

        def piece(tiles, j0, width):
            start = max(first for first in tiles if first <= j0)
            return tiles[start][:, j0 - start : j0 - start + width]

        def gather(tiles, window, j0, width):
            nc.vector.tensor_copy(piece(tiles, j0, width), window.indirect(offsets[:, j0 // 16 : (j0 + width) // 16]))

        def gather_scales(j0, width):
            gather(frame_planes, table_plane[:].bitcast(U8), j0, width)

        def gather_words(j0, width):
            gather(frame_words, table[:].bitcast(U32), j0, width)

        def frames(j0, width):
            return piece(frame_words, j0, width).bitcast(FP8X4), piece(frame_planes, j0, width)

        packed = {
            (name, b): (sbuf([P, PASS], U32, "words_%s%d" % (name, b)), sbuf([P, PASS], U8, "plane_%s%d" % (name, b)))
            for name in ("co", "si")
            for b in range(2)
        }
        rounded = {key: sbuf([P, 2, 2, P, PACK], BF16, "rounded_%s%d" % key) for key in packed if key != ("si", 1)}
        shared = sbuf([P, J * PACK], BF16, "shared")
        rounded["si", 1] = shared[:, PASS : 5 * PASS].rearrange("p (u e m i) -> p u e m i", u=2, e=2, i=PACK)

        def weight(name, b, c0, width):
            words, plane = packed[name, b]
            return words[:, c0 : c0 + width].bitcast(FP8X4), plane[:, c0 : c0 + width]

        def quantize(dst, src):
            nc.vector.quantize_mx(out=dst[0], scales=dst[1], in_=src)

        def quantize_by_pairs(name, b):
            for pair in range(2):
                quantize(weight(name, b, pair * HALF, HALF), rounded[name, b][:, pair].rearrange("p e m i -> p (e m i)"))

        def cast_views(name, b):
            return (
                rounded[name, b][:, :].rearrange("p u e m i -> p u m i e"),
                raw[name, b].rearrange("p i (m u e) -> p u m i e", u=2, e=2),
            )

        def prepare_by_pairs(name, b):
            dst, src = cast_views(name, b)
            for pair in range(2):
                nc.vector.tensor_copy(dst[:, pair], src[:, pair])
            quantize_by_pairs(name, b)

        taken = []

        def next_bank(shape):
            taken.append(shape)
            return sums.tile(shape, F32, name="bank%d" % (len(taken) % SUM_BANKS))

        def product(dst, stationary, moving, start=True, stop=True):
            nc.tensor.matmul_mx(
                out=dst,
                lhsT=stationary[0],
                lhsT_scale=stationary[1],
                rhs=moving[0],
                rhs_scale=moving[1],
                start=start,
                stop=stop,
            )

        by_frame = {}

        def square_by_frame(name, b, jt):
            bank = next_bank([P, PACK, P])
            product(bank[:].rearrange("p t m -> p (t m)"), frames(jt * P, P), weight(name, b, 0, PASS))
            tile = sbuf([P, PACK, P], F32, "by_frame_%s%d_%d" % (name, b, jt))
            by_frame[name, b, jt] = tile[:]
            nc.scalar.activation(tile[:], bank[:], ACT.Square)

        turning = {}

        def turn(names, b, jt):
            opens = (b, jt) not in turning
            if opens:
                turning[b, jt] = turns.tile([P, PACK, P], F32, name="turn%d" % (len(turning) % TURN_BANKS))
            steps = [(name, t) for name in names for t in range(PACK)]
            for step in steps:
                nc.tensor.matmul(
                    turning[b, jt][:, step[1], :],
                    by_frame[step[0], b, jt][:, step[1], :],
                    identity[:],
                    start=opens and step == steps[0],
                    stop="si" in names and step == steps[-1],
                    is_transpose=True,
                )

        def scale_turned(dst, b, jt):
            nc.vector.tensor_tensor(
                dst,
                turning[b, jt][:].rearrange("p t j -> p j t"),
                gain[:, b].unsqueeze(1).to_broadcast([P, P, PACK]),
                ALU.mult,
            )

        squares = {}

        def square_slots(b, j0, width, parts, bank=None):
            if (b, j0) not in squares:
                squares[b, j0] = sbuf([P, 2, width // LINE, PACK, LINE], F32, "squares%d_%d" % (b, j0))
            if bank is None:
                bank = next_bank([P, len(parts), width])
            for place, (name, t) in enumerate(parts):
                product(bank[:, place], weight(name, b, t * P, P), frames(j0, width))
            for t in sorted(set(slot for name, slot in parts)):
                places = [place for place, part in enumerate(parts) if part[1] == t]
                first = ("co", "si").index(parts[places[0]][0])
                nc.scalar.activation(
                    squares[b, j0][:, first : first + len(places), :, t, :].rearrange("p s c i -> p (s c) i"),
                    bank[:, places[0] : places[-1] + 1].rearrange("p s (c i) -> p (s c) i", i=LINE),
                    ACT.Square,
                    scale=root[:, b * PACK + t : b * PACK + t + 1],
                )

        def square_unit(b, j0):
            for t in range(PACK):
                square_slots(b, j0, 256, [("co", t), ("si", t)])

        def add(engine, dst, b, j0, first):
            rows = slice(first // LINE, (first + dst.shape[1]) // LINE)
            engine.tensor_tensor(
                dst.rearrange("p (c i) t -> p c t i", i=LINE),
                squares[b, j0][:, 0, rows],
                squares[b, j0][:, 1, rows],
                ALU.add,
            )

        def apply_sign(dst, src, b):
            signs = sign[:, b * PACK : (b + 1) * PACK].unsqueeze(1).to_broadcast(list(dst.shape))
            nc.vector.tensor_tensor(dst, src, signs, ALU.mult)

        def rounded_power(width, name, tag=None):
            return sbuf([P, width, PACK], BF16, name, tag)[:]

        power_words = [sbuf([P, J], U32, "power_words%d" % b) for b in range(2)]
        power_plane = [sbuf([P, J], U8, "power_plane%d" % b) for b in range(2)]

        def power_codes(b, j0, width):
            return power_words[b][:, j0 : j0 + width].bitcast(FP8X4), power_plane[b][:, j0 : j0 + width]

        def quantize_power(src, b, j0):
            quantize(power_codes(b, j0, src.shape[1]), src.rearrange("p j t -> p (j t)"))

        def filters(b, nt):
            if b == 0:
                codes = fb8[:, nt * P : (nt + 1) * P].bitcast(FP8X4)
            else:
                codes = fb4[:].bitcast(U8)[:, nt * 2 * P : (nt + 1) * 2 * P].bitcast(FP4X4)
            return codes, fb_plane[:].bitcast(U8)[:, b * N + nt * P : b * N + (nt + 1) * P]

        def filter_bank(j0, width, engine_copy):
            acc = next_bank([P, N // P, width])
            steps = [(b, nt) for b in range(2) for nt in range(N // P)]
            for b, nt in steps:
                product(acc[:, nt], filters(b, nt), power_codes(b, j0, width), (b, nt) == steps[0], (b, nt) == steps[-1])
            staged = sbuf([P, N // P, width], F32, "staged%d" % j0)
            engine_copy(staged[:], acc[:])
            nc.sync.dma_start(out=out.rearrange("(a p) j -> p a j", p=P)[:, :, j0 : j0 + width], in_=staged[:])

        def filter_last(j0):
            accs = [turns.tile([P, P], F32, name="turn%d" % nt) for nt in range(N // P)]
            for b in range(2):
                for nt in range(N // P):
                    product(accs[nt][:], filters(b, nt), power_codes(b, j0, P), b == 0, b == 1)
            for nt, engine_copy in enumerate((nc.scalar.copy, nc.vector.tensor_copy)):
                staged = sbuf([P, P], F32, "last%d" % nt)
                engine_copy(staged[:], accs[nt][:])
                nc.sync.dma_start(out=out[nt * P : (nt + 1) * P, j0 : j0 + P], in_=staged[:])

        frame_planes[0] = sbuf([P, J], U8, "frame_plane0")
        gather_scales(0, J)
        for h in range(2):
            nc.scalar.copy(
                rounded["co", 0][:, :, :, h * 64 : (h + 1) * 64, :].rearrange("p u e m i -> p m i (u e)"),
                raw_half[h][:].rearrange("p i (m t) -> p m i t", t=PACK),
            )
        quantize_by_pairs("co", 0)
        by_band = spread[:, :, 0:2].rearrange("p t b -> p b t")
        size = sbuf([P, 2 * PACK], F32, "size")
        sign = sbuf([P, 2 * PACK], BF16, "sign")
        root = sbuf([P, 2 * PACK], F32, "root", "rounded_co0")
        nc.scalar.activation(size[:].rearrange("p (b t) -> p b t", b=2), by_band, ACT.Abs)
        nc.scalar.activation(sign[:].rearrange("p (b t) -> p b t", b=2), by_band, ACT.Sign)
        nc.scalar.copy(gain[:], by_band)
        nc.gpsimd.tensor_tensor(root[:], size[:], half_power[:], ALU.pow)
        for j0, width in ((256, P), (384, P), (512, 256), (0, 256)):
            frame_words[j0] = sbuf([P, width], U32, "frame_words%d" % j0)
            gather_words(j0, width)
        prepare_by_pairs("si", 0)
        frame_words[768] = sbuf([P, 256], U32, "frame_words768", "raw_si0")
        gather_words(768, 256)
        prepare_by_pairs("co", 1)

        for jt in range(2, 6):
            square_by_frame("co", 0, jt)
        for t0 in (0, 2):
            square_slots(0, 0, 256, [("co", t0), ("co", t0 + 1)])
        square_slots(0, 0, 256, [("si", 0), ("si", 1)])
        square_slots(0, 0, 256, [("si", 2), ("si", 3)], turns.tile([P, 2, 256], F32, name="turn2"))
        for jt in range(2, 5):
            turn(("co",), 0, jt)
        power = [
            shared[:].rearrange("p (j t) -> p j t", t=PACK),
            rounded_power(J, "power1"),
        ]

        def scale_tile(b, jt):
            scale_turned(power[b][:, jt * P : (jt + 1) * P], b, jt)

        def quantize_frames(b, j0, width):
            quantize_power(power[b][:, j0 : j0 + width], b, j0)

        def add_frames(engine, b, j0, first, width):
            add(engine, power[b][:, j0 + first : j0 + first + width], b, j0, first)

        def sign_frames(b, j0, width):
            apply_sign(power[b][:, j0 : j0 + width], power[b][:, j0 : j0 + width], b)

        add_frames(nc.vector, 0, 0, 0, OWN_EARLY)
        prepare_by_pairs("si", 1)
        for jt in range(2, 6):
            square_by_frame("si", 0, jt)
        square_unit(0, 768)
        for jt in range(2, 5):
            turn(("si",), 0, jt)
        add_frames(nc.gpsimd, 0, 0, OWN_EARLY, 256 - OWN_EARLY)
        for jt in range(2, 5):
            scale_tile(0, jt)
        turn(("co", "si"), 0, 5)
        sign_frames(0, 0, 256)
        quantize_frames(0, 256, 384)
        quantize_frames(0, 0, 256)
        add_frames(nc.vector, 0, 768, 0, OWN)
        handed = power[0][:, : 256 - OWN]
        add(nc.gpsimd, handed, 0, 768, OWN)
        fourth = power[0][:, P : 2 * P]
        scale_turned(fourth, 0, 5)

        def square_tile(jt):
            for name in ("co", "si"):
                square_by_frame(name, 1, jt)

        def square_single(j0):
            for t0 in (0, 2):
                square_slots(1, j0, P, [(name, t) for t in (t0, t0 + 1) for name in ("co", "si")])

        def square_pair(t):
            square_slots(1, 0, 256, [("co", t), ("si", t)])

        for t in range(3):
            if t < 2:
                square_tile(4 + t)
                square_pair(t)
            else:
                square_single(256)
                square_pair(t)
            if t >= 1:
                turn(("co", "si"), 1, 3 + t)
                scale_tile(1, 3 + t)
            if t == 1:
                sign_frames(0, 768, OWN)
                apply_sign(power[0][:, 768 + OWN :], handed, 0)
                quantize_power(fourth, 0, 640)
        square_pair(3)
        square_tile(3)
        square_tile(6)
        square_single(896)
        turn(("co", "si"), 1, 3)
        turn(("co", "si"), 1, 6)

        quantize_frames(0, 768, 256)
        add_frames(nc.vector, 1, 256, 0, P)
        quantize_frames(1, 512, 256)
        add_frames(nc.vector, 1, 0, 0, 256)
        sign_frames(1, 256, P)
        sign_frames(1, 0, 256)
        quantize_frames(1, 256, P)
        quantize_frames(1, 0, 256)
        scale_tile(1, 3)
        scale_tile(1, 6)
        quantize_frames(1, 384, P)
        add_frames(nc.vector, 1, 896, 0, P)
        quantize_frames(1, 768, P)
        sign_frames(1, 896, P)
        quantize_frames(1, 896, P)
        for j0, width in ((512, 256), (256, P), (0, 256), (384, P)):
            filter_bank(j0, width, nc.scalar.copy)
        filter_bank(768, P, nc.vector.tensor_copy)
        filter_last(896)
